import numpy as np
import ml_dtypes


def mxq(x, axis, fmt="e4m3"):
    dtype, down = {"e4m3": (ml_dtypes.float8_e4m3fn, 7), "e5m2": (ml_dtypes.float8_e5m2, 14)}[fmt]
    v = np.moveaxis(np.asarray(x, np.float32).astype(ml_dtypes.bfloat16).astype(np.float64), axis, -1)
    blocks = v.reshape(v.shape[:-1] + (-1, 32))
    amax = np.abs(blocks).max(-1, keepdims=True)
    byte = np.maximum(np.where(amax > 0, np.frexp(amax)[1] - 1 + 127, 0) - down, 1)
    scale = np.exp2(byte - 127.0)
    codes = (blocks / scale).astype(np.float32).astype(dtype).astype(np.float64)
    return np.moveaxis((codes * scale).reshape(v.shape), -1, axis)


WIDE = False


def mx_kscale(k):
    if not WIDE:
        return np.ones(k)
    levels = np.array([24, -24, 12, -12, 0])
    if k % 512:
        return np.exp2(np.random.permutation(np.resize(levels, k // 32))).repeat(32)
    a = np.empty((k // 512, 16))
    for p in range(k // 512):
        a[p, :8] = np.random.permutation(np.resize(levels, 8))
        for g in range(8):
            far = levels[np.abs(levels - a[p, g]) >= 10]
            a[p, g + 8] = far[np.random.randint(len(far))]
    return np.exp2(a.ravel()).repeat(32)


def f64(x):
    return np.asarray(x).astype(np.float64)


def striped(idx):
    return np.tile(idx.reshape(-1, 16).T, (8, 1)).astype(np.uint16)


def unstriped(offs):
    return offs[:16].T.reshape(-1).astype(np.int64)


E2M1 = np.array([0.0, 0.5, 1.0, 1.5, 2.0, 3.0, 4.0, 6.0, -0.0, -0.5, -1.0, -1.5, -2.0, -3.0, -4.0, -6.0])


def pack_weight(w, fmt):
    k, n = w.shape
    w = f64(np.asarray(w, np.float32).astype(ml_dtypes.bfloat16)).reshape(k // 32, 32, n)
    amax = np.abs(w).max(1)
    if fmt == "e4m3":
        byte = np.frexp(amax)[1] - 1 + 127 - 7
    else:
        mant, ex = np.frexp(amax / 6.0)
        byte = np.where(mant > 0.5, ex, ex - 1) + 127
    byte = np.clip(np.where(amax > 0, byte, 1), 1, 254)
    scaled = (w * np.exp2(127.0 - byte)[:, None, :]).reshape(k, n).astype(np.float32)
    by_word = np.ascontiguousarray(scaled.reshape(k // 512, 128, 4, n).transpose(0, 1, 3, 2))
    if fmt == "e4m3":
        words = by_word.astype(ml_dtypes.float8_e4m3fn).view(np.uint8)
    else:
        c = by_word.astype(ml_dtypes.float4_e2m1fn).view(np.uint8) & 0xF
        words = (c[..., 0::2] | (c[..., 1::2] << 4)).reshape(k // 512, 128, 2 * n)
    return np.ascontiguousarray(words), np.ascontiguousarray(byte.astype(np.uint8).reshape(k // 512, 16, n))


def unpack_weight(words, scales, fmt):
    g, _, n = scales.shape
    words = np.ascontiguousarray(words).reshape(g, 128, n, -1)
    if fmt == "e4m3":
        vals = words.view(ml_dtypes.float8_e4m3fn).astype(np.float64)
    else:
        nib = np.empty((g, 128, n, 4), np.uint8)
        nib[..., 0::2] = words & 0xF
        nib[..., 1::2] = words >> 4
        vals = E2M1[nib]
    vals = vals * np.repeat(np.exp2(scales.astype(np.float64) - 127.0), 8, axis=1)[..., None]
    return vals.transpose(0, 1, 3, 2).reshape(g * 512, n)


def pack_table4(v):
    words, scales = pack_weight(v, "e2m1")
    g, t = words.shape[0] // 2, v.shape[1]
    return np.ascontiguousarray(words.reshape(g, 2, 128, t, 2).transpose(0, 2, 3, 1, 4).reshape(g, 128, t, 4)), scales


def unpack_table4(words, scales):
    g, _, t, _ = words.shape
    return unpack_weight(words.reshape(g, 128, t, 2, 2).transpose(0, 3, 1, 2, 4).reshape(2 * g, 128, 2 * t), scales, "e2m1")


def sigm(f):
    return 1.0 / (1.0 + np.exp(-np.maximum(f, -700.0)))


K, R, N, T, J = 1024, 512, 512, 2048, 1024


def setup_inputs():
    n = np.random.standard_normal
    s = mx_kscale(K)[:, None]
    u = mx_kscale(R)[:, None]
    p_tab = pack_table4(n((K, T)) * s)
    p_wg = pack_weight(n((K, R)) / np.sqrt(K) / s, "e2m1")
    p_wd = pack_weight(n((R, N)) / np.sqrt(R) / u, "e2m1")
    return {
        "tab_words": p_tab[0],
        "tab_scales": p_tab[1],
        "wg_words": p_wg[0],
        "wg_scales": p_wg[1],
        "wu": (n((K, R)) / np.sqrt(K) / s * u.T).astype(np.float32),
        "wd_words": p_wd[0],
        "wd_scales": p_wd[1],
        "rT": (n((N, T))).astype(np.float32),
        "wgo": np.tile(np.random.uniform(0.5, 2.0, J), (128, 1)).astype(np.float32),
        "offs": striped(np.random.permutation(T)[:J]),
    }


def reference(tab_words, tab_scales, wg_words, wg_scales, wu, wd_words, wd_scales, rT, wgo, offs):
    idx = unstriped(offs)
    tab_ = unpack_table4(tab_words, tab_scales)[:, idx]
    wg_ = unpack_weight(wg_words, wg_scales, "e2m1")
    wu_ = mxq(f64(wu), 0, "e4m3")
    ga = wg_.T @ tab_
    ub = wu_.T @ tab_
    h = sigm(ga) * ub
    h_ = mxq(h, 0, "e4m3")
    wd_ = unpack_weight(wd_words, wd_scales, "e2m1")
    y = wd_.T @ h_
    out = np.zeros((N, T))
    out[:, idx] = f64(wgo)[0] * (y + f64(rT)[:, idx])
    return out

@@ -1,0 +1,218 @@
+from contextlib import ExitStack
+
+import concourse.mybir as mybir
+
+K, R, N, T, J = 1024, 512, 512, 2048, 1024
+FLOPS = 2 * (2 * K * R * J + R * N * J)
+
+F32 = mybir.dt.float32
+BF16 = mybir.dt.bfloat16
+I32 = mybir.dt.int32
+U32 = mybir.dt.uint32
+U16 = mybir.dt.uint16
+U8 = mybir.dt.uint8
+FP8X4 = mybir.dt.float8_e4m3fn_x4
+FP4X4 = mybir.dt.float4_e2m1fn_x4
+MULT = mybir.AluOpType.mult
+ADD = mybir.AluOpType.add
+SIGMOID = mybir.ActivationFunctionType.Sigmoid
+
+P = 128
+PACK = 4
+PASSES = K // (P * PACK)
+HALF = J // 2
+CHUNK = 128
+LIST_ROWS = 16
+
+
+def tile_list_modp_gsigm_res_kernel(
+    tc, tab_words, tab_scales, wg_words, wg_scales, wu, wd_words, wd_scales, rT, wgo, offs, out
+):
+    nc = tc.nc
+    with ExitStack() as ctx:
+        keep = ctx.enter_context(tc.tile_pool(name="keep", bufs=1))
+        psum = ctx.enter_context(tc.psum_pool(name="psum", bufs=1))
+
+        def tile(name, shape, dtype):
+            return keep.tile(shape, dtype, name=name, align_bytes=64)
+
+        def half_of_list(h):
+            cols = HALF // LIST_ROWS
+            return offsets[:, h * cols : (h + 1) * cols]
+
+        offsets = keep.tile([P, J // LIST_ROWS], U16, name="offsets")
+        nc.sync.dma_start(offsets[:], offs)
+
+        tab_sc = tile("tab_sc", [P, T], U8)
+        for q in range(4):
+            nc.gpsimd.memset(tab_sc[32 * q : 32 * q + 24, :].bitcast(I32), 0)
+            nc.sync.dma_start(
+                out=tab_sc[32 * q + 24 : 32 * q + 32, :].bitcast(I32),
+                in_=tab_scales[:, 4 * q : 4 * q + 4, :].bitcast(I32),
+            )
+        wg_sc_raw = tile("wg_sc_raw", [P, PASSES * R], U8)
+        nc.vector.memset(wg_sc_raw[:].bitcast(I32), 0)
+        wd_sc = tile("wd_sc", [P, N], U8)
+        nc.gpsimd.memset(wd_sc[:].bitcast(I32), 0)
+        x_sc = [tile("x_sc%d" % a, [P, J], U8) for a in range(PASSES)]
+        for plane in x_sc:
+            nc.gpsimd.memset(plane[:].bitcast(I32), 0)
+        pages = [tile("page%d" % i, [P, T], F32) for i in range(2)]
+        for page in pages:
+            nc.vector.memset(page[:], 0.0)
+
+        warm = tile("warm", [P, 1], F32)
+        nc.scalar.activation(warm[:], pages[0][:, 0:1], SIGMOID)
+
+        tab_w = tile("tab_w", [P, T], I32)
+        nc.sync.dma_start(out=tab_w[:], in_=tab_words[0].rearrange("p t b -> p (t b)").bitcast(I32))
+        wu_raw = {}
+
+        def load_wu(a, c):
+            wu_raw[a, c] = tile("wu_raw%d%d" % (a, c), [P, PACK, R // 2], F32)
+            rows = wu[512 * a : 512 * (a + 1), 256 * c : 256 * (c + 1)]
+            nc.sync.dma_start(out=wu_raw[a, c][:], in_=rows.rearrange("(p i) r -> p i r", i=PACK))
+
+        load_wu(0, 0)
+        load_wu(0, 1)
+        wg_w_raw = tile("wg_w_raw", [P, PASSES, 2 * R], U8)
+        nc.sync.dma_start(out=wg_w_raw[:].bitcast(I32), in_=wg_words.rearrange("a p b -> p a b").bitcast(I32))
+        for q in range(4):
+            nc.sync.dma_start(
+                out=wg_sc_raw[32 * q : 32 * q + 4, :].rearrange("p (a r) -> p a r", a=PASSES).bitcast(I32),
+                in_=wg_scales[:, 4 * q : 4 * q + 4, :].rearrange("a q r -> q a r").bitcast(I32),
+            )
+        load_wu(1, 0)
+        load_wu(1, 1)
+        wd_w = tile("wd_w", [P, 2 * N], U8)
+        nc.sync.dma_start(out=wd_w[:].bitcast(I32), in_=wd_words[0].bitcast(I32))
+        for q in range(4):
+            nc.sync.dma_start(
+                out=wd_sc[32 * q : 32 * q + 4, :].bitcast(I32), in_=wd_scales[0, 4 * q : 4 * q + 4, :].bitcast(I32)
+            )
+        res = [tile("res%d" % n, [P, T], F32) for n in range(N // P)]
+        weight = tile("weight", [P, J], F32)
+        nc.sync.dma_start(out=res[0][:], in_=rT[0:P, :])
+        nc.sync.dma_start(out=weight[:], in_=wgo)
+        for n in range(1, N // P):
+            nc.sync.dma_start(out=res[n][:], in_=rT[n * P : (n + 1) * P, :])
+
+        picked_sc = tile("picked_sc", [P, J], U8)
+        nc.vector.tensor_copy(picked_sc[:], tab_sc[:].indirect(offsets[:]))
+        for a in range(PASSES):
+            first = 24 + 4 * a
+            nc.scalar.dma_start(out=x_sc[a][0:100, :].bitcast(I32), in_=picked_sc[first : first + 100, :].bitcast(I32))
+        pairs, x_w = [], []
+        for h in range(2):
+            pairs.append(tile("pairs%d" % h, [P, HALF], U32))
+            nc.vector.tensor_copy(pairs[h][:], tab_w[:].bitcast(U32).indirect(half_of_list(h)))
+        for h in range(2):
+            x_w.append(tile("x_w%d" % h, [P, PASSES * 2 * HALF], U8))
+            nc.vector.tensor_copy(
+                x_w[h][:].bitcast(U16).rearrange("p (a j) -> p a j", a=PASSES),
+                pairs[h][:].bitcast(U16).rearrange("p (j a) -> p a j", a=PASSES),
+            )
+
+        wg_w = tile("wg_w", [P, PASSES * 2 * R], U8)
+        nc.vector.tensor_copy(
+            wg_w[:].bitcast(U16).rearrange("p (a t m) -> p a t m", a=PASSES, t=PACK),
+            wg_w_raw[:].bitcast(U16).rearrange("p a (m t) -> p a t m", t=PACK),
+        )
+        wg_sc = tile("wg_sc", [P, PASSES * R], U8)
+        nc.vector.tensor_copy(
+            wg_sc[:].rearrange("p (a t m) -> p a t m", a=PASSES, t=PACK),
+            wg_sc_raw[:].rearrange("p (a m t) -> p a t m", a=PASSES, t=PACK),
+        )
+
+        wu_w, wu_sc = [], []
+        for a in range(PASSES):
+            grouped = tile("wu_bf%d" % a, [P, PACK * R], BF16)
+            by_slot = grouped[:].rearrange("p (t c m i) -> p c m t i", t=PACK, c=2, i=PACK)
+            for c in range(2):
+                nc.scalar.copy(by_slot[:, c], wu_raw[a, c][:].rearrange("p i (m t) -> p m t i", t=PACK))
+            wu_w.append(tile("wu_w%d" % a, [P, R], U32))
+            wu_sc.append(tile("wu_sc%d" % a, [P, R], U8))
+            nc.vector.quantize_mx(out=wu_w[a][:].bitcast(FP8X4), scales=wu_sc[a][:], in_=grouped[:])
+
+        def first_stage(bank, c, lhs, lhs_sc):
+            h, j0 = divmod(c * CHUNK, HALF)
+            for a in range(PASSES):
+                for t in range(PACK):
+                    b0 = 2 * (a * HALF + j0)
+                    nc.tensor.matmul_mx(
+                        out=bank[:, t, :],
+                        lhsT=lhs(a, t),
+                        lhsT_scale=lhs_sc(a, t),
+                        rhs=x_w[h][:, b0 : b0 + 2 * CHUNK].bitcast(FP4X4),
+                        rhs_scale=x_sc[a][:, c * CHUNK : (c + 1) * CHUNK],
+                        start=(a == 0 and t == 0),
+                        stop=(a == PASSES - 1 and t == PACK - 1),
+                    )
+
+        h_w = [tile("h_w%d" % h, [P, HALF], U32) for h in range(2)]
+        h_sc = [tile("h_sc%d" % h, [P, HALF], U8) for h in range(2)]
+        y = {}
+
+        def hidden(pair):
+            h_bf = tile("h_bf%d" % pair, [P, 2 * CHUNK * PACK], BF16)
+            for e in range(2):
+                c = 2 * pair + e
+                ga = psum.tile([P, PACK, CHUNK], F32, name="ga", tag="ga", bufs=3)
+                first_stage(
+                    ga,
+                    c,
+                    lambda a, t: wg_w[:, 2 * (a * R + t * P) : 2 * (a * R + (t + 1) * P)].bitcast(FP4X4),
+                    lambda a, t: wg_sc[:, a * R + t * P : a * R + (t + 1) * P],
+                )
+                ub = psum.tile([P, PACK, CHUNK], F32, name="ub", tag="ub", bufs=3)
+                first_stage(
+                    ub,
+                    c,
+                    lambda a, t: wu_w[a][:, t * P : (t + 1) * P].bitcast(FP8X4),
+                    lambda a, t: wu_sc[a][:, t * P : (t + 1) * P],
+                )
+                gate = tile("gate%d" % c, [P, CHUNK, PACK], F32)
+                nc.scalar.activation(gate[:], ga[:].rearrange("p t j -> p j t"), SIGMOID)
+                nc.vector.tensor_tensor(
+                    h_bf[:, e * CHUNK * PACK : (e + 1) * CHUNK * PACK].rearrange("p (j t) -> p j t", t=PACK),
+                    ub[:].rearrange("p t j -> p j t"),
+                    gate[:],
+                    MULT,
+                )
+            h, j0 = divmod(pair * 2 * CHUNK, HALF)
+            cols = slice(j0, j0 + 2 * CHUNK)
+            nc.vector.quantize_mx(out=h_w[h][:, cols].bitcast(FP8X4), scales=h_sc[h][:, cols], in_=h_bf[:])
+
+        def second_stage(h):
+            for n in range(N // P):
+                acc = psum.tile([P, HALF], F32, name="acc", tag="acc", bufs=2)
+                nc.tensor.matmul_mx(
+                    out=acc[:],
+                    lhsT=wd_w[:, 2 * n * P : 2 * (n + 1) * P].bitcast(FP4X4),
+                    lhsT_scale=wd_sc[:, n * P : (n + 1) * P],
+                    rhs=h_w[h][:].bitcast(FP8X4),
+                    rhs_scale=h_sc[h][:],
+                    start=True,
+                    stop=True,
+                )
+                y[n, h] = tile("y%d%d" % (n, h), [P, HALF], F32)
+                nc.scalar.copy(y[n, h][:], acc[:])
+
+        for h in range(2):
+            hidden(2 * h)
+            hidden(2 * h + 1)
+            second_stage(h)
+
+        for n0 in range(0, N // P, 2):
+            for h in range(2):
+                total = {}
+                for n in (n0, n0 + 1):
+                    total[n] = tile("total%d%d" % (n, h), [P, HALF], F32)
+                    nc.vector.tensor_tensor(total[n][:], res[n][:].indirect(half_of_list(h)), y[n, h][:], ADD)
+                for n in (n0, n0 + 1):
+                    page = pages[n % 2]
+                    nc.vector.tensor_tensor(
+                        page[:].indirect(half_of_list(h)), total[n][:], weight[:, h * HALF : (h + 1) * HALF], MULT
+                    )
+                    if h == 1:
+                        nc.sync.dma_start(out=out[n * P : (n + 1) * P, :], in_=page[:])

@@ -33,8 +33,8 @@ def tile_list_modp_gsigm_res_kernel(
         keep = ctx.enter_context(tc.tile_pool(name="keep", bufs=1))
         psum = ctx.enter_context(tc.psum_pool(name="psum", bufs=1))
 
-        def tile(name, shape, dtype):
-            return keep.tile(shape, dtype, name=name, align_bytes=64)
+        def tile(name, shape, dtype, after=None):
+            return keep.tile(shape, dtype, name=name, tag=after or name, align_bytes=64)
 
         def half_of_list(h):
             cols = HALF // LIST_ROWS
@@ -43,29 +43,34 @@ def tile_list_modp_gsigm_res_kernel(
         offsets = keep.tile([P, J // LIST_ROWS], U16, name="offsets")
         nc.sync.dma_start(offsets[:], offs)
 
+        wg_sc_raw = tile("wg_sc_raw", [P, PASSES * R], U8)
+        nc.gpsimd.memset(wg_sc_raw[:].bitcast(I32), 0)
+        x_sc = [tile("x_sc%d" % a, [P, J], U8) for a in range(PASSES)]
+        for plane in x_sc:
+            nc.gpsimd.memset(plane[:].bitcast(I32), 0)
         tab_sc = tile("tab_sc", [P, T], U8)
         for q in range(4):
-            nc.gpsimd.memset(tab_sc[32 * q : 32 * q + 24, :].bitcast(I32), 0)
+            nc.vector.memset(tab_sc[32 * q : 32 * q + 24, :].bitcast(I32), 0)
             nc.sync.dma_start(
                 out=tab_sc[32 * q + 24 : 32 * q + 32, :].bitcast(I32),
                 in_=tab_scales[:, 4 * q : 4 * q + 4, :].bitcast(I32),
             )
-        wg_sc_raw = tile("wg_sc_raw", [P, PASSES * R], U8)
-        nc.vector.memset(wg_sc_raw[:].bitcast(I32), 0)
-        wd_sc = tile("wd_sc", [P, N], U8)
-        nc.gpsimd.memset(wd_sc[:].bitcast(I32), 0)
-        x_sc = [tile("x_sc%d" % a, [P, J], U8) for a in range(PASSES)]
-        for plane in x_sc:
-            nc.gpsimd.memset(plane[:].bitcast(I32), 0)
-        pages = [tile("page%d" % i, [P, T], F32) for i in range(2)]
-        for page in pages:
-            nc.vector.memset(page[:], 0.0)
+        pages = [tile("page0", [P, T], F32)]
+        nc.vector.memset(pages[0][:], 0.0)
 
         warm = tile("warm", [P, 1], F32)
-        nc.scalar.activation(warm[:], pages[0][:, 0:1], SIGMOID)
+        nc.gpsimd.memset(warm[:], 0.0)
+        nc.scalar.activation(warm[:], warm[:], SIGMOID)
 
         tab_w = tile("tab_w", [P, T], I32)
         nc.sync.dma_start(out=tab_w[:], in_=tab_words[0].rearrange("p t b -> p (t b)").bitcast(I32))
+        wg_w_raw = tile("wg_w_raw", [P, PASSES, 2 * R], U8)
+        nc.sync.dma_start(out=wg_w_raw[:].bitcast(I32), in_=wg_words.rearrange("a p b -> p a b").bitcast(I32))
+        for q in range(4):
+            nc.sync.dma_start(
+                out=wg_sc_raw[32 * q : 32 * q + 4, :].rearrange("p (a r) -> p a r", a=PASSES).bitcast(I32),
+                in_=wg_scales[:, 4 * q : 4 * q + 4, :].rearrange("a q r -> q a r").bitcast(I32),
+            )
         wu_raw = {}
 
         def load_wu(a, c):
@@ -75,44 +80,28 @@ def tile_list_modp_gsigm_res_kernel(
 
         load_wu(0, 0)
         load_wu(0, 1)
-        wg_w_raw = tile("wg_w_raw", [P, PASSES, 2 * R], U8)
-        nc.sync.dma_start(out=wg_w_raw[:].bitcast(I32), in_=wg_words.rearrange("a p b -> p a b").bitcast(I32))
-        for q in range(4):
-            nc.sync.dma_start(
-                out=wg_sc_raw[32 * q : 32 * q + 4, :].rearrange("p (a r) -> p a r", a=PASSES).bitcast(I32),
-                in_=wg_scales[:, 4 * q : 4 * q + 4, :].rearrange("a q r -> q a r").bitcast(I32),
-            )
         load_wu(1, 0)
         load_wu(1, 1)
-        wd_w = tile("wd_w", [P, 2 * N], U8)
-        nc.sync.dma_start(out=wd_w[:].bitcast(I32), in_=wd_words[0].bitcast(I32))
-        for q in range(4):
-            nc.sync.dma_start(
-                out=wd_sc[32 * q : 32 * q + 4, :].bitcast(I32), in_=wd_scales[0, 4 * q : 4 * q + 4, :].bitcast(I32)
-            )
-        res = [tile("res%d" % n, [P, T], F32) for n in range(N // P)]
-        weight = tile("weight", [P, J], F32)
-        nc.sync.dma_start(out=res[0][:], in_=rT[0:P, :])
-        nc.sync.dma_start(out=weight[:], in_=wgo)
-        for n in range(1, N // P):
-            nc.sync.dma_start(out=res[n][:], in_=rT[n * P : (n + 1) * P, :])
 
         picked_sc = tile("picked_sc", [P, J], U8)
         nc.vector.tensor_copy(picked_sc[:], tab_sc[:].indirect(offsets[:]))
         for a in range(PASSES):
             first = 24 + 4 * a
-            nc.scalar.dma_start(out=x_sc[a][0:100, :].bitcast(I32), in_=picked_sc[first : first + 100, :].bitcast(I32))
-        pairs, x_w = [], []
-        for h in range(2):
-            pairs.append(tile("pairs%d" % h, [P, HALF], U32))
+            nc.sync.dma_start(out=x_sc[a][0:100, :].bitcast(I32), in_=picked_sc[first : first + 100, :].bitcast(I32))
+        pairs, x_w = {}, {}
+
+        def gather_words(h, after=None):
+            pairs[h] = tile("pairs%d" % h, [P, HALF], U32, after=after)
             nc.vector.tensor_copy(pairs[h][:], tab_w[:].bitcast(U32).indirect(half_of_list(h)))
-        for h in range(2):
-            x_w.append(tile("x_w%d" % h, [P, PASSES * 2 * HALF], U8))
+
+        def part_words(h):
+            x_w[h] = tile("x_w%d" % h, [P, PASSES * 2 * HALF], U8)
             nc.vector.tensor_copy(
                 x_w[h][:].bitcast(U16).rearrange("p (a j) -> p a j", a=PASSES),
                 pairs[h][:].bitcast(U16).rearrange("p (j a) -> p a j", a=PASSES),
             )
 
+        gather_words(0)
         wg_w = tile("wg_w", [P, PASSES * 2 * R], U8)
         nc.vector.tensor_copy(
             wg_w[:].bitcast(U16).rearrange("p (a t m) -> p a t m", a=PASSES, t=PACK),
@@ -124,6 +113,7 @@ def tile_list_modp_gsigm_res_kernel(
             wg_sc_raw[:].rearrange("p (a m t) -> p a t m", a=PASSES, t=PACK),
         )
 
+        part_words(0)
         wu_w, wu_sc = [], []
         for a in range(PASSES):
             grouped = tile("wu_bf%d" % a, [P, PACK * R], BF16)
@@ -133,6 +123,27 @@ def tile_list_modp_gsigm_res_kernel(
             wu_w.append(tile("wu_w%d" % a, [P, R], U32))
             wu_sc.append(tile("wu_sc%d" % a, [P, R], U8))
             nc.vector.quantize_mx(out=wu_w[a][:].bitcast(FP8X4), scales=wu_sc[a][:], in_=grouped[:])
+
+        gather_words(1, after="wu_bf0")
+        part_words(1)
+        pages.append(tile("page1", [P, T], F32, after="wu_bf1"))
+        nc.gpsimd.memset(pages[1][:], 0.0)
+
+        wd_w = tile("wd_w", [P, 2 * N], U8, after="tab_sc")
+        nc.sync.dma_start(out=wd_w[:].bitcast(I32), in_=wd_words[0].bitcast(I32))
+        wd_sc = tile("wd_sc", [P, N], U8, after="pairs0")
+        nc.gpsimd.memset(wd_sc[:].bitcast(I32), 0)
+        for q in range(4):
+            nc.sync.dma_start(
+                out=wd_sc[32 * q : 32 * q + 4, :].bitcast(I32), in_=wd_scales[0, 4 * q : 4 * q + 4, :].bitcast(I32)
+            )
+        res = []
+        for n, freed in enumerate(("wu_raw00", "wu_raw10", "wu_raw11", "tab_w")):
+            res.append(tile("res%d" % n, [P, T], F32, after=freed))
+            nc.sync.dma_start(out=res[n][:], in_=rT[n * P : (n + 1) * P, :])
+            if n == 0:
+                weight = tile("weight", [P, J], F32, after="wu_raw01")
+                nc.sync.dma_start(out=weight[:], in_=wgo)
 
         def first_stage(bank, c, lhs, lhs_sc):
             h, j0 = divmod(c * CHUNK, HALF)
@@ -149,9 +160,8 @@ def tile_list_modp_gsigm_res_kernel(
                         stop=(a == PASSES - 1 and t == PACK - 1),
                     )
 
-        h_w = [tile("h_w%d" % h, [P, HALF], U32) for h in range(2)]
-        h_sc = [tile("h_sc%d" % h, [P, HALF], U8) for h in range(2)]
-        y = {}
+        h_w = tile("h_w", [P, J], U32)
+        h_sc = tile("h_sc", [P, J], U8)
 
         def hidden(pair):
             h_bf = tile("h_bf%d" % pair, [P, 2 * CHUNK * PACK], BF16)
@@ -179,40 +189,50 @@ def tile_list_modp_gsigm_res_kernel(
                     gate[:],
                     MULT,
                 )
-            h, j0 = divmod(pair * 2 * CHUNK, HALF)
-            cols = slice(j0, j0 + 2 * CHUNK)
-            nc.vector.quantize_mx(out=h_w[h][:, cols].bitcast(FP8X4), scales=h_sc[h][:, cols], in_=h_bf[:])
+            cols = slice(pair * 2 * CHUNK, (pair + 1) * 2 * CHUNK)
+            nc.vector.quantize_mx(out=h_w[:, cols].bitcast(FP8X4), scales=h_sc[:, cols], in_=h_bf[:])
 
-        def second_stage(h):
-            for n in range(N // P):
-                acc = psum.tile([P, HALF], F32, name="acc", tag="acc", bufs=2)
-                nc.tensor.matmul_mx(
-                    out=acc[:],
-                    lhsT=wd_w[:, 2 * n * P : 2 * (n + 1) * P].bitcast(FP4X4),
-                    lhsT_scale=wd_sc[:, n * P : (n + 1) * P],
-                    rhs=h_w[h][:].bitcast(FP8X4),
-                    rhs_scale=h_sc[h][:],
-                    start=True,
-                    stop=True,
-                )
-                y[n, h] = tile("y%d%d" % (n, h), [P, HALF], F32)
-                nc.scalar.copy(y[n, h][:], acc[:])
+        y = [tile("y%d" % n, [P, J], F32) for n in range(N // P)]
 
-        for h in range(2):
-            hidden(2 * h)
-            hidden(2 * h + 1)
-            second_stage(h)
+        def second_stage(n, j0, j1):
+            acc = psum.tile([P, j1 - j0], F32, name="acc", tag="acc", bufs=2)
+            nc.tensor.matmul_mx(
+                out=acc[:],
+                lhsT=wd_w[:, 2 * n * P : 2 * (n + 1) * P].bitcast(FP4X4),
+                lhsT_scale=wd_sc[:, n * P : (n + 1) * P],
+                rhs=h_w[:, j0:j1].bitcast(FP8X4),
+                rhs_scale=h_sc[:, j0:j1],
+                start=True,
+                stop=True,
+            )
+            nc.scalar.copy(y[n][:, j0:j1], acc[:])
 
-        for n0 in range(0, N // P, 2):
-            for h in range(2):
-                total = {}
-                for n in (n0, n0 + 1):
-                    total[n] = tile("total%d%d" % (n, h), [P, HALF], F32)
-                    nc.vector.tensor_tensor(total[n][:], res[n][:].indirect(half_of_list(h)), y[n, h][:], ADD)
-                for n in (n0, n0 + 1):
-                    page = pages[n % 2]
-                    nc.vector.tensor_tensor(
-                        page[:].indirect(half_of_list(h)), total[n][:], weight[:, h * HALF : (h + 1) * HALF], MULT
-                    )
-                    if h == 1:
-                        nc.sync.dma_start(out=out[n * P : (n + 1) * P, :], in_=page[:])
+        def place(rows, j0, j1):
+            entries = offsets[:, j0 // LIST_ROWS : j1 // LIST_ROWS]
+            total = {}
+            for n in rows:
+                total[n] = tile("total%d_%d" % (n, j0), [P, j1 - j0], F32)
+                nc.vector.tensor_tensor(total[n][:], res[n][:].indirect(entries), y[n][:, j0:j1], ADD)
+            for n in rows:
+                page = pages[n % 2]
+                nc.vector.tensor_tensor(page[:].indirect(entries), total[n][:], weight[:, j0:j1], MULT)
+                if j1 == J:
+                    nc.sync.dma_start(out=out[n * P : (n + 1) * P, :], in_=page[:])
+
+        EARLY = 2 * CHUNK
+        hidden(0)
+        for n in (0, 1):
+            second_stage(n, 0, EARLY)
+        hidden(1)
+        for n in (0, 1):
+            second_stage(n, EARLY, HALF)
+        hidden(2)
+        hidden(3)
+        for n in (0, 1):
+            second_stage(n, HALF, J)
+        for n in (2, 3):
+            second_stage(n, 0, HALF)
+            second_stage(n, HALF, J)
+        place((0, 1), 0, EARLY)
+        place((0, 1), EARLY, J)
+        place((2, 3), 0, J)

@@ -19,10 +19,20 @@ SIGMOID = mybir.ActivationFunctionType.Sigmoid
 
 P = 128
 PACK = 4
-PASSES = K // (P * PACK)
+K_PASS = P * PACK
+PASSES = K // K_PASS
+QUAD = 32
+QUADS = P // QUAD
+SC_ROWS = 4
+FP4_BYTES = 2
+LIST_ROWS = 16
+ROW_BLOCKS = N // P
 HALF = J // 2
 CHUNK = 128
-LIST_ROWS = 16
+PAIR = 2 * CHUNK
+TAB_SC_FIRST = QUAD - PASSES * SC_ROWS
+SC_SPAN = (QUADS - 1) * QUAD + SC_ROWS
+WU_PIECES = (((0, 256), (256, 512)), ((0, 256), (256, 384), (384, 512)))
 
 
 def tile_list_modp_gsigm_res_kernel(
@@ -33,76 +43,58 @@ def tile_list_modp_gsigm_res_kernel(
         keep = ctx.enter_context(tc.tile_pool(name="keep", bufs=1))
         psum = ctx.enter_context(tc.psum_pool(name="psum", bufs=1))
 
-        def tile(name, shape, dtype, after=None):
-            return keep.tile(shape, dtype, name=name, tag=after or name, align_bytes=64)
-
-        def half_of_list(h):
-            cols = HALF // LIST_ROWS
-            return offsets[:, h * cols : (h + 1) * cols]
+        def tile(name, shape, dtype, reuse=None):
+            return keep.tile(shape, dtype, name=name, tag=reuse or name, align_bytes=64)
 
         offsets = keep.tile([P, J // LIST_ROWS], U16, name="offsets")
         nc.sync.dma_start(offsets[:], offs)
 
+        def entries(j0, j1):
+            return offsets[:, j0 // LIST_ROWS : j1 // LIST_ROWS]
+
         wg_sc_raw = tile("wg_sc_raw", [P, PASSES * R], U8)
         nc.gpsimd.memset(wg_sc_raw[:].bitcast(I32), 0)
         x_sc = [tile("x_sc%d" % a, [P, J], U8) for a in range(PASSES)]
-        for plane in x_sc:
-            nc.gpsimd.memset(plane[:].bitcast(I32), 0)
+        for a in range(PASSES):
+            nc.gpsimd.memset(x_sc[a][:].bitcast(I32), 0)
         tab_sc = tile("tab_sc", [P, T], U8)
-        for q in range(4):
-            nc.vector.memset(tab_sc[32 * q : 32 * q + 24, :].bitcast(I32), 0)
+        for q in range(QUADS):
+            nc.vector.memset(tab_sc[QUAD * q : QUAD * q + TAB_SC_FIRST, :].bitcast(I32), 0)
             nc.sync.dma_start(
-                out=tab_sc[32 * q + 24 : 32 * q + 32, :].bitcast(I32),
-                in_=tab_scales[:, 4 * q : 4 * q + 4, :].bitcast(I32),
+                out=tab_sc[QUAD * q + TAB_SC_FIRST : QUAD * (q + 1), :].bitcast(I32),
+                in_=tab_scales[:, SC_ROWS * q : SC_ROWS * (q + 1), :].bitcast(I32),
             )
-        pages = [tile("page0", [P, T], F32)]
-        nc.vector.memset(pages[0][:], 0.0)
 
-        warm = tile("warm", [P, 1], F32)
-        nc.gpsimd.memset(warm[:], 0.0)
-        nc.scalar.activation(warm[:], warm[:], SIGMOID)
-
-        tab_w = tile("tab_w", [P, T], I32)
-        nc.sync.dma_start(out=tab_w[:], in_=tab_words[0].rearrange("p t b -> p (t b)").bitcast(I32))
-        wg_w_raw = tile("wg_w_raw", [P, PASSES, 2 * R], U8)
-        nc.sync.dma_start(out=wg_w_raw[:].bitcast(I32), in_=wg_words.rearrange("a p b -> p a b").bitcast(I32))
-        for q in range(4):
-            nc.sync.dma_start(
-                out=wg_sc_raw[32 * q : 32 * q + 4, :].rearrange("p (a r) -> p a r", a=PASSES).bitcast(I32),
-                in_=wg_scales[:, 4 * q : 4 * q + 4, :].rearrange("a q r -> q a r").bitcast(I32),
-            )
         wu_raw = {}
 
-        def load_wu(a, c):
-            wu_raw[a, c] = tile("wu_raw%d%d" % (a, c), [P, PACK, R // 2], F32)
-            rows = wu[512 * a : 512 * (a + 1), 256 * c : 256 * (c + 1)]
-            nc.sync.dma_start(out=wu_raw[a, c][:], in_=rows.rearrange("(p i) r -> p i r", i=PACK))
+        def load_wu(a):
+            for r0, r1 in WU_PIECES[a]:
+                wu_raw[a, r0] = tile("wu_raw%d_%d" % (a, r0), [P, PACK, r1 - r0], F32)
+                rows = wu[K_PASS * a : K_PASS * (a + 1), r0:r1]
+                nc.sync.dma_start(out=wu_raw[a, r0][:], in_=rows.rearrange("(p i) r -> p i r", i=PACK))
 
-        load_wu(0, 0)
-        load_wu(0, 1)
-        load_wu(1, 0)
-        load_wu(1, 1)
+        load_wu(0)
+        wg_w_raw = tile("wg_w_raw", [P, PASSES, FP4_BYTES * R], U8)
+        nc.sync.dma_start(out=wg_w_raw[:].bitcast(I32), in_=wg_words.rearrange("a p b -> p a b").bitcast(I32))
+        for q in range(QUADS):
+            rows = wg_sc_raw[QUAD * q : QUAD * q + SC_ROWS, :]
+            nc.sync.dma_start(
+                out=rows.rearrange("p (a r) -> p a r", a=PASSES).bitcast(I32),
+                in_=wg_scales[:, SC_ROWS * q : SC_ROWS * (q + 1), :].rearrange("a q r -> q a r").bitcast(I32),
+            )
+        tab_w = tile("tab_w", [P, T], I32)
+        nc.sync.dma_start(out=tab_w[:], in_=tab_words[0].rearrange("p t b -> p (t b)").bitcast(I32))
+        load_wu(1)
 
         picked_sc = tile("picked_sc", [P, J], U8)
         nc.vector.tensor_copy(picked_sc[:], tab_sc[:].indirect(offsets[:]))
         for a in range(PASSES):
-            first = 24 + 4 * a
-            nc.sync.dma_start(out=x_sc[a][0:100, :].bitcast(I32), in_=picked_sc[first : first + 100, :].bitcast(I32))
-        pairs, x_w = {}, {}
-
-        def gather_words(h, after=None):
-            pairs[h] = tile("pairs%d" % h, [P, HALF], U32, after=after)
-            nc.vector.tensor_copy(pairs[h][:], tab_w[:].bitcast(U32).indirect(half_of_list(h)))
-
-        def part_words(h):
-            x_w[h] = tile("x_w%d" % h, [P, PASSES * 2 * HALF], U8)
-            nc.vector.tensor_copy(
-                x_w[h][:].bitcast(U16).rearrange("p (a j) -> p a j", a=PASSES),
-                pairs[h][:].bitcast(U16).rearrange("p (j a) -> p a j", a=PASSES),
+            first = TAB_SC_FIRST + SC_ROWS * a
+            nc.sync.dma_start(
+                out=x_sc[a][0:SC_SPAN, :].bitcast(I32), in_=picked_sc[first : first + SC_SPAN, :].bitcast(I32)
             )
 
-        gather_words(0)
-        wg_w = tile("wg_w", [P, PASSES * 2 * R], U8)
+        wg_w = tile("wg_w", [P, PASSES * FP4_BYTES * R], U8)
         nc.vector.tensor_copy(
             wg_w[:].bitcast(U16).rearrange("p (a t m) -> p a t m", a=PASSES, t=PACK),
             wg_w_raw[:].bitcast(U16).rearrange("p a (m t) -> p a t m", t=PACK),
@@ -113,48 +105,68 @@ def tile_list_modp_gsigm_res_kernel(
             wg_sc_raw[:].rearrange("p (a m t) -> p a t m", a=PASSES, t=PACK),
         )
 
-        part_words(0)
+        x_w = []
+
+        def pick_words(half):
+            both = tile("both%d" % half, [P, HALF], U32, reuse="both")
+            nc.vector.tensor_copy(both[:], tab_w[:].bitcast(U32).indirect(entries(half * HALF, (half + 1) * HALF)))
+            x_w.append(tile("x_w%d" % half, [P, PASSES * FP4_BYTES * HALF], U8))
+            nc.vector.tensor_copy(
+                x_w[half][:].bitcast(U16).rearrange("p (a j) -> p a j", a=PASSES),
+                both[:].bitcast(U16).rearrange("p (j a) -> p a j", a=PASSES),
+            )
+
+        pick_words(0)
+
         wu_w, wu_sc = [], []
         for a in range(PASSES):
-            grouped = tile("wu_bf%d" % a, [P, PACK * R], BF16)
-            by_slot = grouped[:].rearrange("p (t c m i) -> p c m t i", t=PACK, c=2, i=PACK)
-            for c in range(2):
-                nc.scalar.copy(by_slot[:, c], wu_raw[a, c][:].rearrange("p i (m t) -> p m t i", t=PACK))
+            wu_bf = tile("wu_bf%d" % a, [P, PACK * R], BF16)
+            by_slot = wu_bf[:].rearrange("p (t m i) -> p m t i", t=PACK, i=PACK)
+            for r0, r1 in WU_PIECES[a]:
+                nc.scalar.copy(
+                    by_slot[:, r0 // PACK : r1 // PACK], wu_raw[a, r0][:].rearrange("p i (m t) -> p m t i", t=PACK)
+                )
             wu_w.append(tile("wu_w%d" % a, [P, R], U32))
             wu_sc.append(tile("wu_sc%d" % a, [P, R], U8))
-            nc.vector.quantize_mx(out=wu_w[a][:].bitcast(FP8X4), scales=wu_sc[a][:], in_=grouped[:])
+            nc.vector.quantize_mx(out=wu_w[a][:].bitcast(FP8X4), scales=wu_sc[a][:], in_=wu_bf[:])
 
-        gather_words(1, after="wu_bf0")
-        part_words(1)
-        pages.append(tile("page1", [P, T], F32, after="wu_bf1"))
-        nc.gpsimd.memset(pages[1][:], 0.0)
+        pick_words(1)
 
-        wd_w = tile("wd_w", [P, 2 * N], U8, after="tab_sc")
+        pages = [tile("page0", [P, T], F32, reuse="wu_bf1")]
+        nc.vector.memset(pages[0][:].bitcast(I32), 0)
+
+        wd_w = tile("wd_w", [P, FP4_BYTES * N], U8, reuse="tab_sc")
         nc.sync.dma_start(out=wd_w[:].bitcast(I32), in_=wd_words[0].bitcast(I32))
-        wd_sc = tile("wd_sc", [P, N], U8, after="pairs0")
+        wd_sc = tile("wd_sc", [P, N], U8, reuse="wu_bf0")
         nc.gpsimd.memset(wd_sc[:].bitcast(I32), 0)
-        for q in range(4):
+        for q in range(QUADS):
             nc.sync.dma_start(
-                out=wd_sc[32 * q : 32 * q + 4, :].bitcast(I32), in_=wd_scales[0, 4 * q : 4 * q + 4, :].bitcast(I32)
+                out=wd_sc[QUAD * q : QUAD * q + SC_ROWS, :].bitcast(I32),
+                in_=wd_scales[0, SC_ROWS * q : SC_ROWS * (q + 1), :].bitcast(I32),
             )
         res = []
-        for n, freed in enumerate(("wu_raw00", "wu_raw10", "wu_raw11", "tab_w")):
-            res.append(tile("res%d" % n, [P, T], F32, after=freed))
-            nc.sync.dma_start(out=res[n][:], in_=rT[n * P : (n + 1) * P, :])
-            if n == 0:
-                weight = tile("weight", [P, J], F32, after="wu_raw01")
-                nc.sync.dma_start(out=weight[:], in_=wgo)
 
-        def first_stage(bank, c, lhs, lhs_sc):
-            h, j0 = divmod(c * CHUNK, HALF)
+        def load_res(n, reuse):
+            res.append(tile("res%d" % n, [P, T], F32, reuse=reuse))
+            nc.sync.dma_start(out=res[n][:], in_=rT[n * P : (n + 1) * P, :])
+
+        load_res(0, "wg_w_raw")
+        weight = tile("weight", [P, J], F32, reuse="wg_sc_raw")
+        nc.sync.dma_start(out=weight[:], in_=wgo)
+        load_res(1, "wu_raw1_0")
+        load_res(2, "wu_raw1_384")
+        load_res(3, "tab_w")
+
+        def first_product(bank, c, words, scales):
+            half, j0 = divmod(c * CHUNK, HALF)
             for a in range(PASSES):
+                b0 = FP4_BYTES * (a * HALF + j0)
                 for t in range(PACK):
-                    b0 = 2 * (a * HALF + j0)
                     nc.tensor.matmul_mx(
                         out=bank[:, t, :],
-                        lhsT=lhs(a, t),
-                        lhsT_scale=lhs_sc(a, t),
-                        rhs=x_w[h][:, b0 : b0 + 2 * CHUNK].bitcast(FP4X4),
+                        lhsT=words(a, t),
+                        lhsT_scale=scales(a, t),
+                        rhs=x_w[half][:, b0 : b0 + FP4_BYTES * CHUNK].bitcast(FP4X4),
                         rhs_scale=x_sc[a][:, c * CHUNK : (c + 1) * CHUNK],
                         start=(a == 0 and t == 0),
                         stop=(a == PASSES - 1 and t == PACK - 1),
@@ -164,18 +176,18 @@ def tile_list_modp_gsigm_res_kernel(
         h_sc = tile("h_sc", [P, J], U8)
 
         def hidden(pair):
-            h_bf = tile("h_bf%d" % pair, [P, 2 * CHUNK * PACK], BF16)
-            for e in range(2):
-                c = 2 * pair + e
+            h_bf = tile("h_bf%d" % pair, [P, PAIR * PACK], BF16)
+            for e in range(PAIR // CHUNK):
+                c = pair * (PAIR // CHUNK) + e
                 ga = psum.tile([P, PACK, CHUNK], F32, name="ga", tag="ga", bufs=3)
-                first_stage(
+                first_product(
                     ga,
                     c,
-                    lambda a, t: wg_w[:, 2 * (a * R + t * P) : 2 * (a * R + (t + 1) * P)].bitcast(FP4X4),
+                    lambda a, t: wg_w[:, FP4_BYTES * (a * R + t * P) : FP4_BYTES * (a * R + (t + 1) * P)].bitcast(FP4X4),
                     lambda a, t: wg_sc[:, a * R + t * P : a * R + (t + 1) * P],
                 )
                 ub = psum.tile([P, PACK, CHUNK], F32, name="ub", tag="ub", bufs=3)
-                first_stage(
+                first_product(
                     ub,
                     c,
                     lambda a, t: wu_w[a][:, t * P : (t + 1) * P].bitcast(FP8X4),
@@ -189,16 +201,16 @@ def tile_list_modp_gsigm_res_kernel(
                     gate[:],
                     MULT,
                 )
-            cols = slice(pair * 2 * CHUNK, (pair + 1) * 2 * CHUNK)
+            cols = slice(pair * PAIR, (pair + 1) * PAIR)
             nc.vector.quantize_mx(out=h_w[:, cols].bitcast(FP8X4), scales=h_sc[:, cols], in_=h_bf[:])
 
-        y = [tile("y%d" % n, [P, J], F32) for n in range(N // P)]
+        y = [tile("y%d" % n, [P, J], F32) for n in range(ROW_BLOCKS)]
 
-        def second_stage(n, j0, j1):
+        def second_product(n, j0, j1):
             acc = psum.tile([P, j1 - j0], F32, name="acc", tag="acc", bufs=2)
             nc.tensor.matmul_mx(
                 out=acc[:],
-                lhsT=wd_w[:, 2 * n * P : 2 * (n + 1) * P].bitcast(FP4X4),
+                lhsT=wd_w[:, FP4_BYTES * n * P : FP4_BYTES * (n + 1) * P].bitcast(FP4X4),
                 lhsT_scale=wd_sc[:, n * P : (n + 1) * P],
                 rhs=h_w[:, j0:j1].bitcast(FP8X4),
                 rhs_scale=h_sc[:, j0:j1],
@@ -207,32 +219,37 @@ def tile_list_modp_gsigm_res_kernel(
             )
             nc.scalar.copy(y[n][:, j0:j1], acc[:])
 
-        def place(rows, j0, j1):
-            entries = offsets[:, j0 // LIST_ROWS : j1 // LIST_ROWS]
-            total = {}
-            for n in rows:
-                total[n] = tile("total%d_%d" % (n, j0), [P, j1 - j0], F32)
-                nc.vector.tensor_tensor(total[n][:], res[n][:].indirect(entries), y[n][:, j0:j1], ADD)
-            for n in rows:
-                page = pages[n % 2]
-                nc.vector.tensor_tensor(page[:].indirect(entries), total[n][:], weight[:, j0:j1], MULT)
-                if j1 == J:
-                    nc.sync.dma_start(out=out[n * P : (n + 1) * P, :], in_=page[:])
+        def add_residual(n, j0, j1):
+            nc.vector.tensor_tensor(total[n][:, j0:j1], res[n][:].indirect(entries(j0, j1)), y[n][:, j0:j1], ADD)
 
-        EARLY = 2 * CHUNK
-        hidden(0)
-        for n in (0, 1):
-            second_stage(n, 0, EARLY)
-        hidden(1)
-        for n in (0, 1):
-            second_stage(n, EARLY, HALF)
-        hidden(2)
-        hidden(3)
-        for n in (0, 1):
-            second_stage(n, HALF, J)
-        for n in (2, 3):
-            second_stage(n, 0, HALF)
-            second_stage(n, HALF, J)
-        place((0, 1), 0, EARLY)
-        place((0, 1), EARLY, J)
-        place((2, 3), 0, J)
+        def place(n, j0, j1):
+            page = pages[n % 2]
+            nc.vector.tensor_tensor(page[:].indirect(entries(j0, j1)), total[n][:, j0:j1], weight[:, j0:j1], MULT)
+            if j1 == J:
+                nc.sync.dma_start(out=out[n * P : (n + 1) * P, :], in_=page[:])
+
+        last = ROW_BLOCKS - 1
+        total = [tile("total%d" % n, [P, J], F32) for n in range(last)]
+        for pair in range(HALF // PAIR):
+            j0, j1 = pair * PAIR, (pair + 1) * PAIR
+            hidden(pair)
+            second_product(0, j0, j1)
+            add_residual(0, j0, j1)
+            place(0, j0, j1)
+        for n in range(1, ROW_BLOCKS):
+            second_product(n, 0, HALF)
+        for pair in range(HALF // PAIR, J // PAIR):
+            hidden(pair)
+        total.append(tile("total%d" % last, [P, J], F32, reuse="h_bf%d" % (J // PAIR - 1)))
+        for n in range(1, ROW_BLOCKS):
+            add_residual(n, 0, HALF)
+
+        for n in range(ROW_BLOCKS):
+            second_product(n, HALF, J)
+        pages.append(tile("page1", [P, T], F32, reuse="h_w"))
+        nc.gpsimd.memset(pages[1][:], 0.0)
+        add_residual(0, HALF, J)
+        for n in range(ROW_BLOCKS):
+            if n < last:
+                add_residual(n + 1, HALF, J)
+            place(n, HALF if n == 0 else 0, J)

@@ -29,7 +29,7 @@ LIST_ROWS = 16
 ROW_BLOCKS = N // P
 HALF = J // 2
 CHUNK = 128
-PAIR = 2 * CHUNK
+VECTOR_CHUNKS = 2
 TAB_SC_FIRST = QUAD - PASSES * SC_ROWS
 SC_SPAN = (QUADS - 1) * QUAD + SC_ROWS
 WU_PIECES = (((0, 256), (256, 512)), ((0, 256), (256, 384), (384, 512)))
@@ -54,16 +54,19 @@ def tile_list_modp_gsigm_res_kernel(
 
         wg_sc_raw = tile("wg_sc_raw", [P, PASSES * R], U8)
         nc.gpsimd.memset(wg_sc_raw[:].bitcast(I32), 0)
-        x_sc = [tile("x_sc%d" % a, [P, J], U8) for a in range(PASSES)]
-        for a in range(PASSES):
-            nc.gpsimd.memset(x_sc[a][:].bitcast(I32), 0)
         tab_sc = tile("tab_sc", [P, T], U8)
         for q in range(QUADS):
-            nc.vector.memset(tab_sc[QUAD * q : QUAD * q + TAB_SC_FIRST, :].bitcast(I32), 0)
+            nc.gpsimd.memset(tab_sc[QUAD * q : QUAD * q + TAB_SC_FIRST, :].bitcast(I32), 0)
             nc.sync.dma_start(
                 out=tab_sc[QUAD * q + TAB_SC_FIRST : QUAD * (q + 1), :].bitcast(I32),
                 in_=tab_scales[:, SC_ROWS * q : SC_ROWS * (q + 1), :].bitcast(I32),
             )
+
+        x_sc = [tile("x_sc%d" % a, [P, J], U8) for a in range(PASSES)]
+        for a in range(PASSES):
+            nc.gpsimd.memset(x_sc[a][:].bitcast(I32), 0)
+        pages = [tile("page0", [P, T], F32)]
+        nc.gpsimd.memset(pages[0][:], 0.0)
 
         wu_raw = {}
 
@@ -132,8 +135,9 @@ def tile_list_modp_gsigm_res_kernel(
 
         pick_words(1)
 
-        pages = [tile("page0", [P, T], F32, reuse="wu_bf1")]
-        nc.vector.memset(pages[0][:].bitcast(I32), 0)
+        pages.append(tile("page1", [P, T], F32, reuse="wu_bf1"))
+        for c0 in range(0, T, HALF):
+            nc.gpsimd.memset(pages[1][:, c0 : c0 + HALF], 0.0)
 
         wd_w = tile("wd_w", [P, FP4_BYTES * N], U8, reuse="tab_sc")
         nc.sync.dma_start(out=wd_w[:].bitcast(I32), in_=wd_words[0].bitcast(I32))
@@ -175,81 +179,104 @@ def tile_list_modp_gsigm_res_kernel(
         h_w = tile("h_w", [P, J], U32)
         h_sc = tile("h_sc", [P, J], U8)
 
-        def hidden(pair):
-            h_bf = tile("h_bf%d" % pair, [P, PAIR * PACK], BF16)
-            for e in range(PAIR // CHUNK):
-                c = pair * (PAIR // CHUNK) + e
-                ga = psum.tile([P, PACK, CHUNK], F32, name="ga", tag="ga", bufs=3)
-                first_product(
-                    ga,
-                    c,
-                    lambda a, t: wg_w[:, FP4_BYTES * (a * R + t * P) : FP4_BYTES * (a * R + (t + 1) * P)].bitcast(FP4X4),
-                    lambda a, t: wg_sc[:, a * R + t * P : a * R + (t + 1) * P],
-                )
-                ub = psum.tile([P, PACK, CHUNK], F32, name="ub", tag="ub", bufs=3)
-                first_product(
-                    ub,
-                    c,
-                    lambda a, t: wu_w[a][:, t * P : (t + 1) * P].bitcast(FP8X4),
-                    lambda a, t: wu_sc[a][:, t * P : (t + 1) * P],
-                )
-                gate = tile("gate%d" % c, [P, CHUNK, PACK], F32)
-                nc.scalar.activation(gate[:], ga[:].rearrange("p t j -> p j t"), SIGMOID)
-                nc.vector.tensor_tensor(
-                    h_bf[:, e * CHUNK * PACK : (e + 1) * CHUNK * PACK].rearrange("p (j t) -> p j t", t=PACK),
-                    ub[:].rearrange("p t j -> p j t"),
-                    gate[:],
-                    MULT,
-                )
-            cols = slice(pair * PAIR, (pair + 1) * PAIR)
-            nc.vector.quantize_mx(out=h_w[:, cols].bitcast(FP8X4), scales=h_sc[:, cols], in_=h_bf[:])
+        h_bf = [tile("h_bf%d" % half, [P, HALF * PACK], BF16) for half in range(2)]
 
-        y = [tile("y%d" % n, [P, J], F32) for n in range(ROW_BLOCKS)]
+        def hidden(c):
+            ga = psum.tile([P, PACK, CHUNK], F32, name="ga", tag="ga", bufs=3)
+            first_product(
+                ga,
+                c,
+                lambda a, t: wg_w[:, FP4_BYTES * (a * R + t * P) : FP4_BYTES * (a * R + (t + 1) * P)].bitcast(FP4X4),
+                lambda a, t: wg_sc[:, a * R + t * P : a * R + (t + 1) * P],
+            )
+            ub = psum.tile([P, PACK, CHUNK], F32, name="ub", tag="ub", bufs=3)
+            first_product(
+                ub,
+                c,
+                lambda a, t: wu_w[a][:, t * P : (t + 1) * P].bitcast(FP8X4),
+                lambda a, t: wu_sc[a][:, t * P : (t + 1) * P],
+            )
+            gate = tile("gate%d" % c, [P, CHUNK, PACK], F32)
+            nc.scalar.activation(gate[:], ga[:].rearrange("p t j -> p j t"), SIGMOID)
+            half, j0 = divmod(c * CHUNK, HALF)
+            h = h_bf[half][:, j0 * PACK : (j0 + CHUNK) * PACK].rearrange("p (j t) -> p j t", t=PACK)
+            if c < VECTOR_CHUNKS:
+                nc.vector.tensor_tensor(h, ub[:].rearrange("p t j -> p j t"), gate[:], MULT)
+            else:
+                up = tile("up%d" % c, [P, CHUNK, PACK], F32)
+                nc.scalar.copy(up[:], ub[:].rearrange("p t j -> p j t"))
+                nc.gpsimd.tensor_tensor(h, up[:], gate[:], MULT)
 
-        def second_product(n, j0, j1):
-            acc = psum.tile([P, j1 - j0], F32, name="acc", tag="acc", bufs=2)
+        def quantise_h(half):
+            cols = slice(half * HALF, (half + 1) * HALF)
+            nc.vector.quantize_mx(out=h_w[:, cols].bitcast(FP8X4), scales=h_sc[:, cols], in_=h_bf[half][:])
+
+        y = {}
+
+        def second_product(n, half):
+            cols = slice(half * HALF, (half + 1) * HALF)
+            acc = psum.tile([P, HALF], F32, name="acc", tag="acc", bufs=2)
             nc.tensor.matmul_mx(
                 out=acc[:],
                 lhsT=wd_w[:, FP4_BYTES * n * P : FP4_BYTES * (n + 1) * P].bitcast(FP4X4),
                 lhsT_scale=wd_sc[:, n * P : (n + 1) * P],
-                rhs=h_w[:, j0:j1].bitcast(FP8X4),
-                rhs_scale=h_sc[:, j0:j1],
+                rhs=h_w[:, cols].bitcast(FP8X4),
+                rhs_scale=h_sc[:, cols],
                 start=True,
                 stop=True,
             )
-            nc.scalar.copy(y[n][:, j0:j1], acc[:])
+            y[n, half] = tile("y%d_%d" % (n, half), [P, HALF], F32)
+            nc.scalar.copy(y[n, half][:], acc[:])
 
-        def add_residual(n, j0, j1):
-            nc.vector.tensor_tensor(total[n][:, j0:j1], res[n][:].indirect(entries(j0, j1)), y[n][:, j0:j1], ADD)
+        picked = {}
+
+        def pick_residual(n, reuse=None):
+            picked[n] = tile("picked%d" % n, [P, J], F32, reuse=reuse)
+            nc.vector.tensor_copy(picked[n][:], res[n][:].indirect(offsets[:]))
+
+        scaled = [tile("scaled%d" % n, [P, J], F32) for n in range(ROW_BLOCKS)]
+
+        def combine(n, half):
+            cols = slice(half * HALF, (half + 1) * HALF)
+            total = tile("total%d_%d" % (n, half), [P, HALF], F32)
+            nc.gpsimd.tensor_tensor(total[:], picked[n][:, cols], y[n, half][:], ADD)
+            nc.gpsimd.tensor_tensor(scaled[n][:, cols], total[:], weight[:, cols], MULT)
 
         def place(n, j0, j1):
             page = pages[n % 2]
-            nc.vector.tensor_tensor(page[:].indirect(entries(j0, j1)), total[n][:, j0:j1], weight[:, j0:j1], MULT)
+            nc.vector.tensor_copy(page[:].indirect(entries(j0, j1)), scaled[n][:, j0:j1])
             if j1 == J:
                 nc.sync.dma_start(out=out[n * P : (n + 1) * P, :], in_=page[:])
 
-        last = ROW_BLOCKS - 1
-        total = [tile("total%d" % n, [P, J], F32) for n in range(last)]
-        for pair in range(HALF // PAIR):
-            j0, j1 = pair * PAIR, (pair + 1) * PAIR
-            hidden(pair)
-            second_product(0, j0, j1)
-            add_residual(0, j0, j1)
-            place(0, j0, j1)
-        for n in range(1, ROW_BLOCKS):
-            second_product(n, 0, HALF)
-        for pair in range(HALF // PAIR, J // PAIR):
-            hidden(pair)
-        total.append(tile("total%d" % last, [P, J], F32, reuse="h_bf%d" % (J // PAIR - 1)))
-        for n in range(1, ROW_BLOCKS):
-            add_residual(n, 0, HALF)
-
-        for n in range(ROW_BLOCKS):
-            second_product(n, HALF, J)
-        pages.append(tile("page1", [P, T], F32, reuse="h_w"))
-        nc.gpsimd.memset(pages[1][:], 0.0)
-        add_residual(0, HALF, J)
-        for n in range(ROW_BLOCKS):
-            if n < last:
-                add_residual(n + 1, HALF, J)
-            place(n, HALF if n == 0 else 0, J)
+        hidden(0)
+        hidden(1)
+        pick_residual(0)
+        hidden(2)
+        hidden(3)
+        pick_residual(1)
+        quantise_h(0)
+        hidden(4)
+        second_product(0, 0)
+        pick_residual(2, reuse="h_bf0")
+        hidden(5)
+        combine(0, 0)
+        hidden(6)
+        second_product(1, 0)
+        hidden(7)
+        pick_residual(3)
+        quantise_h(1)
+        combine(1, 0)
+        second_product(0, 1)
+        combine(0, 1)
+        second_product(1, 1)
+        combine(1, 1)
+        for n in range(2, ROW_BLOCKS):
+            for half in range(2):
+                second_product(n, half)
+                combine(n, half)
+        place(0, 0, HALF)
+        place(1, 0, HALF)
+        place(0, HALF, J)
+        place(1, HALF, J)
+        for n in range(2, ROW_BLOCKS):
+            place(n, 0, J)

@@ -29,7 +29,7 @@ LIST_ROWS = 16
 ROW_BLOCKS = N // P
 HALF = J // 2
 CHUNK = 128
-VECTOR_CHUNKS = 2
+VECTOR_CHUNKS = (0, 1, 6, 7)
 TAB_SC_FIRST = QUAD - PASSES * SC_ROWS
 SC_SPAN = (QUADS - 1) * QUAD + SC_ROWS
 WU_PIECES = (((0, 256), (256, 512)), ((0, 256), (256, 384), (384, 512)))
@@ -43,7 +43,11 @@ def tile_list_modp_gsigm_res_kernel(
         keep = ctx.enter_context(tc.tile_pool(name="keep", bufs=1))
         psum = ctx.enter_context(tc.psum_pool(name="psum", bufs=1))
 
+        shared = ctx.enter_context(tc.tile_pool(name="shared", bufs=1))
+
         def tile(name, shape, dtype, reuse=None):
+            if isinstance(reuse, int):
+                return shared.tile(shape, dtype, name=name, offset=reuse, align_bytes=64)
             return keep.tile(shape, dtype, name=name, tag=reuse or name, align_bytes=64)
 
         offsets = keep.tile([P, J // LIST_ROWS], U16, name="offsets")
@@ -65,29 +69,35 @@ def tile_list_modp_gsigm_res_kernel(
         x_sc = [tile("x_sc%d" % a, [P, J], U8) for a in range(PASSES)]
         for a in range(PASSES):
             nc.gpsimd.memset(x_sc[a][:].bitcast(I32), 0)
-        pages = [tile("page0", [P, T], F32)]
-        nc.gpsimd.memset(pages[0][:], 0.0)
+        pages = [tile("page%d" % i, [P, T], F32) for i in range(2)]
+        for page in pages:
+            for c0 in range(0, T, HALF):
+                nc.gpsimd.memset(page[:, c0 : c0 + HALF], 0.0)
+
+        warm = tile("warm", [P, 1], F32)
+        nc.scalar.activation(warm[:], pages[0][:, 0:1], SIGMOID)
 
         wu_raw = {}
 
-        def load_wu(a):
-            for r0, r1 in WU_PIECES[a]:
-                wu_raw[a, r0] = tile("wu_raw%d_%d" % (a, r0), [P, PACK, r1 - r0], F32)
-                rows = wu[K_PASS * a : K_PASS * (a + 1), r0:r1]
-                nc.sync.dma_start(out=wu_raw[a, r0][:], in_=rows.rearrange("(p i) r -> p i r", i=PACK))
+        def load_wu(a, r0, r1, reuse=None):
+            wu_raw[a, r0] = tile("wu_raw%d_%d" % (a, r0), [P, PACK, r1 - r0], F32, reuse=reuse)
+            rows = wu[K_PASS * a : K_PASS * (a + 1), r0:r1]
+            nc.sync.dma_start(out=wu_raw[a, r0][:], in_=rows.rearrange("(p i) r -> p i r", i=PACK))
 
-        load_wu(0)
+        tab_w = tile("tab_w", [P, T], I32)
+        nc.sync.dma_start(out=tab_w[:], in_=tab_words[0].rearrange("p t b -> p (t b)").bitcast(I32))
         wg_w_raw = tile("wg_w_raw", [P, PASSES, FP4_BYTES * R], U8)
         nc.sync.dma_start(out=wg_w_raw[:].bitcast(I32), in_=wg_words.rearrange("a p b -> p a b").bitcast(I32))
+        load_wu(0, *WU_PIECES[0][0])
         for q in range(QUADS):
             rows = wg_sc_raw[QUAD * q : QUAD * q + SC_ROWS, :]
             nc.sync.dma_start(
                 out=rows.rearrange("p (a r) -> p a r", a=PASSES).bitcast(I32),
                 in_=wg_scales[:, SC_ROWS * q : SC_ROWS * (q + 1), :].rearrange("a q r -> q a r").bitcast(I32),
             )
-        tab_w = tile("tab_w", [P, T], I32)
-        nc.sync.dma_start(out=tab_w[:], in_=tab_words[0].rearrange("p t b -> p (t b)").bitcast(I32))
-        load_wu(1)
+        load_wu(0, *WU_PIECES[0][1])
+        for r0, r1 in WU_PIECES[1]:
+            load_wu(1, r0, r1, reuse=0 if r0 == 0 else None)
 
         picked_sc = tile("picked_sc", [P, J], U8)
         nc.vector.tensor_copy(picked_sc[:], tab_sc[:].indirect(offsets[:]))
@@ -96,6 +106,14 @@ def tile_list_modp_gsigm_res_kernel(
             nc.sync.dma_start(
                 out=x_sc[a][0:SC_SPAN, :].bitcast(I32), in_=picked_sc[first : first + SC_SPAN, :].bitcast(I32)
             )
+
+        both = tile("both", [P, J], U32)
+        nc.vector.tensor_copy(both[:], tab_w[:].bitcast(U32).indirect(offsets[:]))
+        x_w = tile("x_w", [P, PASSES * FP4_BYTES * J], U8)
+        nc.vector.tensor_copy(
+            x_w[:].bitcast(U16).rearrange("p (a j) -> p a j", a=PASSES),
+            both[:].bitcast(U16).rearrange("p (j a) -> p a j", a=PASSES),
+        )
 
         wg_w = tile("wg_w", [P, PASSES * FP4_BYTES * R], U8)
         nc.vector.tensor_copy(
@@ -107,19 +125,6 @@ def tile_list_modp_gsigm_res_kernel(
             wg_sc[:].rearrange("p (a t m) -> p a t m", a=PASSES, t=PACK),
             wg_sc_raw[:].rearrange("p (a m t) -> p a t m", a=PASSES, t=PACK),
         )
-
-        x_w = []
-
-        def pick_words(half):
-            both = tile("both%d" % half, [P, HALF], U32, reuse="both")
-            nc.vector.tensor_copy(both[:], tab_w[:].bitcast(U32).indirect(entries(half * HALF, (half + 1) * HALF)))
-            x_w.append(tile("x_w%d" % half, [P, PASSES * FP4_BYTES * HALF], U8))
-            nc.vector.tensor_copy(
-                x_w[half][:].bitcast(U16).rearrange("p (a j) -> p a j", a=PASSES),
-                both[:].bitcast(U16).rearrange("p (j a) -> p a j", a=PASSES),
-            )
-
-        pick_words(0)
 
         wu_w, wu_sc = [], []
         for a in range(PASSES):
@@ -133,94 +138,98 @@ def tile_list_modp_gsigm_res_kernel(
             wu_sc.append(tile("wu_sc%d" % a, [P, R], U8))
             nc.vector.quantize_mx(out=wu_w[a][:].bitcast(FP8X4), scales=wu_sc[a][:], in_=wu_bf[:])
 
-        pick_words(1)
 
-        pages.append(tile("page1", [P, T], F32, reuse="wu_bf1"))
-        for c0 in range(0, T, HALF):
-            nc.gpsimd.memset(pages[1][:, c0 : c0 + HALF], 0.0)
-
-        wd_w = tile("wd_w", [P, FP4_BYTES * N], U8, reuse="tab_sc")
-        nc.sync.dma_start(out=wd_w[:].bitcast(I32), in_=wd_words[0].bitcast(I32))
-        wd_sc = tile("wd_sc", [P, N], U8, reuse="wu_bf0")
-        nc.gpsimd.memset(wd_sc[:].bitcast(I32), 0)
-        for q in range(QUADS):
-            nc.sync.dma_start(
-                out=wd_sc[QUAD * q : QUAD * q + SC_ROWS, :].bitcast(I32),
-                in_=wd_scales[0, SC_ROWS * q : SC_ROWS * (q + 1), :].bitcast(I32),
-            )
         res = []
 
         def load_res(n, reuse):
             res.append(tile("res%d" % n, [P, T], F32, reuse=reuse))
             nc.sync.dma_start(out=res[n][:], in_=rT[n * P : (n + 1) * P, :])
 
-        load_res(0, "wg_w_raw")
-        weight = tile("weight", [P, J], F32, reuse="wg_sc_raw")
+        load_res(0, "tab_sc")
+        wd_w = tile("wd_w", [P, FP4_BYTES * N], U8, reuse="wg_w_raw")
+        nc.sync.dma_start(out=wd_w[:].bitcast(I32), in_=wd_words[0].bitcast(I32))
+        load_res(1, "wu_raw0_0")
+        wd_sc = tile("wd_sc", [P, N], U8, reuse="wg_sc_raw")
+        nc.gpsimd.memset(wd_sc[:].bitcast(I32), 0)
+        for q in range(QUADS):
+            nc.sync.dma_start(
+                out=wd_sc[QUAD * q : QUAD * q + SC_ROWS, :].bitcast(I32),
+                in_=wd_scales[0, SC_ROWS * q : SC_ROWS * (q + 1), :].bitcast(I32),
+            )
+        weight = tile("weight", [P, J], F32, reuse="wu_raw0_256")
         nc.sync.dma_start(out=weight[:], in_=wgo)
-        load_res(1, "wu_raw1_0")
-        load_res(2, "wu_raw1_384")
-        load_res(3, "tab_w")
+        load_res(2, 0)
+        load_res(3, "wu_raw1_384")
 
         def first_product(bank, c, words, scales):
-            half, j0 = divmod(c * CHUNK, HALF)
             for a in range(PASSES):
-                b0 = FP4_BYTES * (a * HALF + j0)
+                b0 = FP4_BYTES * (a * J + c * CHUNK)
                 for t in range(PACK):
                     nc.tensor.matmul_mx(
                         out=bank[:, t, :],
                         lhsT=words(a, t),
                         lhsT_scale=scales(a, t),
-                        rhs=x_w[half][:, b0 : b0 + FP4_BYTES * CHUNK].bitcast(FP4X4),
+                        rhs=x_w[:, b0 : b0 + FP4_BYTES * CHUNK].bitcast(FP4X4),
                         rhs_scale=x_sc[a][:, c * CHUNK : (c + 1) * CHUNK],
                         start=(a == 0 and t == 0),
                         stop=(a == PASSES - 1 and t == PACK - 1),
                     )
 
-        h_w = tile("h_w", [P, J], U32)
+        h_w, h_bf = {}, {}
         h_sc = tile("h_sc", [P, J], U8)
 
-        h_bf = [tile("h_bf%d" % half, [P, HALF * PACK], BF16) for half in range(2)]
+        def bank(shape):
+            return psum.tile(shape, F32, name="bank", tag="bank", bufs=8)
 
-        def hidden(c):
-            ga = psum.tile([P, PACK, CHUNK], F32, name="ga", tag="ga", bufs=3)
+        gate = {}
+
+        def gate_product(c):
+            ga = bank([P, PACK, CHUNK])
             first_product(
                 ga,
                 c,
                 lambda a, t: wg_w[:, FP4_BYTES * (a * R + t * P) : FP4_BYTES * (a * R + (t + 1) * P)].bitcast(FP4X4),
                 lambda a, t: wg_sc[:, a * R + t * P : a * R + (t + 1) * P],
             )
-            ub = psum.tile([P, PACK, CHUNK], F32, name="ub", tag="ub", bufs=3)
+            gate[c] = tile("gate%d" % c, [P, CHUNK, PACK], F32)
+            nc.scalar.activation(gate[c][:], ga[:].rearrange("p t j -> p j t"), SIGMOID)
+
+        def hidden(c, reuse=None):
+            ub = bank([P, PACK, CHUNK])
             first_product(
                 ub,
                 c,
                 lambda a, t: wu_w[a][:, t * P : (t + 1) * P].bitcast(FP8X4),
                 lambda a, t: wu_sc[a][:, t * P : (t + 1) * P],
             )
-            gate = tile("gate%d" % c, [P, CHUNK, PACK], F32)
-            nc.scalar.activation(gate[:], ga[:].rearrange("p t j -> p j t"), SIGMOID)
-            half, j0 = divmod(c * CHUNK, HALF)
-            h = h_bf[half][:, j0 * PACK : (j0 + CHUNK) * PACK].rearrange("p (j t) -> p j t", t=PACK)
-            if c < VECTOR_CHUNKS:
-                nc.vector.tensor_tensor(h, ub[:].rearrange("p t j -> p j t"), gate[:], MULT)
+            first = max(c0 for c0 in h_bf if c0 <= c)
+            j0 = (c - first) * CHUNK
+            h = h_bf[first][:, j0 * PACK : (j0 + CHUNK) * PACK].rearrange("p (j t) -> p j t", t=PACK)
+            if c in VECTOR_CHUNKS:
+                nc.vector.tensor_tensor(h, ub[:].rearrange("p t j -> p j t"), gate[c][:], MULT)
             else:
-                up = tile("up%d" % c, [P, CHUNK, PACK], F32)
+                up = tile("up%d" % c, [P, CHUNK, PACK], F32, reuse=reuse)
                 nc.scalar.copy(up[:], ub[:].rearrange("p t j -> p j t"))
-                nc.gpsimd.tensor_tensor(h, up[:], gate[:], MULT)
+                nc.gpsimd.tensor_tensor(h, up[:], gate[c][:], MULT)
 
-        def quantise_h(half):
-            cols = slice(half * HALF, (half + 1) * HALF)
-            nc.vector.quantize_mx(out=h_w[:, cols].bitcast(FP8X4), scales=h_sc[:, cols], in_=h_bf[half][:])
+        def quantise_h(c0, c1):
+            half, j0 = divmod(c0 * CHUNK, HALF)
+            nc.vector.quantize_mx(
+                out=h_w[half][:, j0 : j0 + (c1 - c0) * CHUNK].bitcast(FP8X4),
+                scales=h_sc[:, c0 * CHUNK : c1 * CHUNK],
+                in_=h_bf[c0][:],
+            )
 
         y = {}
 
         def second_product(n, half):
             cols = slice(half * HALF, (half + 1) * HALF)
-            acc = psum.tile([P, HALF], F32, name="acc", tag="acc", bufs=2)
+            acc = bank([P, HALF])
             nc.tensor.matmul_mx(
                 out=acc[:],
                 lhsT=wd_w[:, FP4_BYTES * n * P : FP4_BYTES * (n + 1) * P].bitcast(FP4X4),
                 lhsT_scale=wd_sc[:, n * P : (n + 1) * P],
-                rhs=h_w[:, cols].bitcast(FP8X4),
+                rhs=h_w[half][:].bitcast(FP8X4),
                 rhs_scale=h_sc[:, cols],
                 start=True,
                 stop=True,
@@ -230,53 +239,75 @@ def tile_list_modp_gsigm_res_kernel(
 
         picked = {}
 
-        def pick_residual(n, reuse=None):
-            picked[n] = tile("picked%d" % n, [P, J], F32, reuse=reuse)
-            nc.vector.tensor_copy(picked[n][:], res[n][:].indirect(offsets[:]))
+        def pick_residual(n, half, reuse=None):
+            picked[n, half] = tile("picked%d_%d" % (n, half), [P, HALF], F32, reuse=reuse)[:]
+            nc.vector.tensor_copy(picked[n, half], res[n][:].indirect(entries(half * HALF, (half + 1) * HALF)))
 
-        scaled = [tile("scaled%d" % n, [P, J], F32) for n in range(ROW_BLOCKS)]
+        def pick_whole(n, reuse=None):
+            whole = tile("picked%d" % n, [P, J], F32, reuse=reuse)
+            nc.vector.tensor_copy(whole[:], res[n][:].indirect(offsets[:]))
+            for half in range(2):
+                picked[n, half] = whole[:, half * HALF : (half + 1) * HALF]
 
-        def combine(n, half):
-            cols = slice(half * HALF, (half + 1) * HALF)
-            total = tile("total%d_%d" % (n, half), [P, HALF], F32)
-            nc.gpsimd.tensor_tensor(total[:], picked[n][:, cols], y[n, half][:], ADD)
-            nc.gpsimd.tensor_tensor(scaled[n][:, cols], total[:], weight[:, cols], MULT)
+        scaled = {}
 
-        def place(n, j0, j1):
+        def combine(n, half, total_reuse=None, scaled_reuse=None, into=None):
+            total = tile("total%d_%d" % (n, half), [P, HALF], F32, reuse=total_reuse)
+            nc.gpsimd.tensor_tensor(total[:], picked[n, half], y[n, half][:], ADD)
+            if into is None:
+                scaled[n, half] = tile("scaled%d_%d" % (n, half), [P, HALF], F32, reuse=scaled_reuse)
+                into = scaled[n, half][:]
+            nc.gpsimd.tensor_tensor(into, total[:], weight[:, half * HALF : (half + 1) * HALF], MULT)
+
+        def place(n, half):
             page = pages[n % 2]
-            nc.vector.tensor_copy(page[:].indirect(entries(j0, j1)), scaled[n][:, j0:j1])
-            if j1 == J:
+            nc.vector.tensor_copy(page[:].indirect(entries(half * HALF, (half + 1) * HALF)), scaled[n, half][:])
+            if half == 1:
                 nc.sync.dma_start(out=out[n * P : (n + 1) * P, :], in_=page[:])
 
+        gate_product(0)
+        gate_product(1)
+        pick_whole(0)
+        h_bf[0] = tile("h_bf0", [P, HALF * PACK], BF16, reuse="tab_sc")
         hidden(0)
         hidden(1)
-        pick_residual(0)
-        hidden(2)
-        hidden(3)
-        pick_residual(1)
-        quantise_h(0)
-        hidden(4)
+        pick_whole(1)
+        for c in (2, 3):
+            gate_product(c)
+            hidden(c)
+        h_w[0] = tile("h_w0", [P, HALF], U32, reuse="wu_raw0_0")
+        quantise_h(0, 4)
+        pick_whole(2, reuse="tab_sc")
+        h_bf[4] = tile("h_bf4", [P, 2 * CHUNK * PACK], BF16)
+        for c in (4, 5):
+            gate_product(c)
+            hidden(c)
+        h_w[1] = tile("h_w1", [P, HALF], U32, reuse=3 * HALF * 4)
+        quantise_h(4, 6)
+        gate_product(6)
         second_product(0, 0)
-        pick_residual(2, reuse="h_bf0")
-        hidden(5)
-        combine(0, 0)
+        h_bf[6] = tile("h_bf6", [P, 2 * CHUNK * PACK], BF16, reuse=HALF * 2)
         hidden(6)
-        second_product(1, 0)
+        gate_product(7)
         hidden(7)
-        pick_residual(3)
-        quantise_h(1)
-        combine(1, 0)
+        second_product(1, 0)
+        quantise_h(6, 8)
+        pick_residual(3, 0, reuse=0)
+        combine(0, 0, scaled_reuse=HALF * 4)
+        place(0, 0)
+        combine(1, 0, scaled_reuse="total0_0")
         second_product(0, 1)
         combine(0, 1)
         second_product(1, 1)
         combine(1, 1)
+        place(1, 0)
+        place(0, 1)
+        pick_residual(3, 1, reuse="scaled0_1")
+        place(1, 1)
         for n in range(2, ROW_BLOCKS):
+            whole = tile("scaled%d" % n, [P, J], F32)
             for half in range(2):
                 second_product(n, half)
-                combine(n, half)
-        place(0, 0, HALF)
-        place(1, 0, HALF)
-        place(0, HALF, J)
-        place(1, HALF, J)
-        for n in range(2, ROW_BLOCKS):
-            place(n, 0, J)
+                combine(n, half, into=whole[:, half * HALF : (half + 1) * HALF])
+            nc.vector.tensor_copy(pages[n % 2][:].indirect(offsets[:]), whole[:])
+            nc.sync.dma_start(out=out[n * P : (n + 1) * P, :], in_=pages[n % 2][:])

@@ -29,7 +29,7 @@ LIST_ROWS = 16
 ROW_BLOCKS = N // P
 HALF = J // 2
 CHUNK = 128
-VECTOR_CHUNKS = (0, 1, 6, 7)
+VECTOR_CHUNKS = (4, 5, 6, 7)
 TAB_SC_FIRST = QUAD - PASSES * SC_ROWS
 SC_SPAN = (QUADS - 1) * QUAD + SC_ROWS
 WU_PIECES = (((0, 256), (256, 512)), ((0, 256), (256, 384), (384, 512)))
@@ -69,10 +69,8 @@ def tile_list_modp_gsigm_res_kernel(
         x_sc = [tile("x_sc%d" % a, [P, J], U8) for a in range(PASSES)]
         for a in range(PASSES):
             nc.gpsimd.memset(x_sc[a][:].bitcast(I32), 0)
-        pages = [tile("page%d" % i, [P, T], F32) for i in range(2)]
-        for page in pages:
-            for c0 in range(0, T, HALF):
-                nc.gpsimd.memset(page[:, c0 : c0 + HALF], 0.0)
+        pages = [tile("page0", [P, T], F32)]
+        nc.gpsimd.memset(pages[0][:], 0.0)
 
         warm = tile("warm", [P, 1], F32)
         nc.scalar.activation(warm[:], pages[0][:, 0:1], SIGMOID)
@@ -95,9 +93,9 @@ def tile_list_modp_gsigm_res_kernel(
                 out=rows.rearrange("p (a r) -> p a r", a=PASSES).bitcast(I32),
                 in_=wg_scales[:, SC_ROWS * q : SC_ROWS * (q + 1), :].rearrange("a q r -> q a r").bitcast(I32),
             )
-        load_wu(0, *WU_PIECES[0][1])
+        load_wu(0, *WU_PIECES[0][1], reuse=0)
         for r0, r1 in WU_PIECES[1]:
-            load_wu(1, r0, r1, reuse=0 if r0 == 0 else None)
+            load_wu(1, r0, r1)
 
         picked_sc = tile("picked_sc", [P, J], U8)
         nc.vector.tensor_copy(picked_sc[:], tab_sc[:].indirect(offsets[:]))
@@ -139,6 +137,9 @@ def tile_list_modp_gsigm_res_kernel(
             nc.vector.quantize_mx(out=wu_w[a][:].bitcast(FP8X4), scales=wu_sc[a][:], in_=wu_bf[:])
 
 
+        pages.append(tile("page1", [P, T], F32, reuse="wu_bf1"))
+        nc.gpsimd.memset(pages[1][:], 0.0)
+
         res = []
 
         def load_res(n, reuse):
@@ -146,20 +147,19 @@ def tile_list_modp_gsigm_res_kernel(
             nc.sync.dma_start(out=res[n][:], in_=rT[n * P : (n + 1) * P, :])
 
         load_res(0, "tab_sc")
-        wd_w = tile("wd_w", [P, FP4_BYTES * N], U8, reuse="wg_w_raw")
-        nc.sync.dma_start(out=wd_w[:].bitcast(I32), in_=wd_words[0].bitcast(I32))
         load_res(1, "wu_raw0_0")
-        wd_sc = tile("wd_sc", [P, N], U8, reuse="wg_sc_raw")
+        load_res(2, 0)
+        wd_w = tile("wd_w", [P, FP4_BYTES * N], U8, reuse="wu_raw1_0")
+        nc.sync.dma_start(out=wd_w[:].bitcast(I32), in_=wd_words[0].bitcast(I32))
+        wd_sc = tile("wd_sc", [P, N], U8, reuse="wu_raw1_256")
         nc.gpsimd.memset(wd_sc[:].bitcast(I32), 0)
         for q in range(QUADS):
             nc.sync.dma_start(
                 out=wd_sc[QUAD * q : QUAD * q + SC_ROWS, :].bitcast(I32),
                 in_=wd_scales[0, SC_ROWS * q : SC_ROWS * (q + 1), :].bitcast(I32),
             )
-        weight = tile("weight", [P, J], F32, reuse="wu_raw0_256")
+        weight = tile("weight", [P, J], F32, reuse="wu_raw1_384")
         nc.sync.dma_start(out=weight[:], in_=wgo)
-        load_res(2, 0)
-        load_res(3, "wu_raw1_384")
 
         def first_product(bank, c, words, scales):
             for a in range(PASSES):
@@ -268,34 +268,29 @@ def tile_list_modp_gsigm_res_kernel(
         gate_product(0)
         gate_product(1)
         pick_whole(0)
-        h_bf[0] = tile("h_bf0", [P, HALF * PACK], BF16, reuse="tab_sc")
+        load_res(3, "tab_sc")
+        h_bf[0] = tile("h_bf0", [P, HALF * PACK], BF16, reuse=T * 4)
         hidden(0)
         hidden(1)
         pick_whole(1)
         for c in (2, 3):
             gate_product(c)
             hidden(c)
-        h_w[0] = tile("h_w0", [P, HALF], U32, reuse="wu_raw0_0")
+        pick_whole(2)
+        h_w[0] = tile("h_w0", [P, HALF], U32, reuse=0)
         quantise_h(0, 4)
-        pick_whole(2, reuse="tab_sc")
-        h_bf[4] = tile("h_bf4", [P, 2 * CHUNK * PACK], BF16)
-        for c in (4, 5):
+        h_bf[4] = tile("h_bf4", [P, HALF * PACK], BF16, reuse=T * 4)
+        for c in (4, 5, 6, 7):
             gate_product(c)
             hidden(c)
-        h_w[1] = tile("h_w1", [P, HALF], U32, reuse=3 * HALF * 4)
-        quantise_h(4, 6)
-        gate_product(6)
         second_product(0, 0)
-        h_bf[6] = tile("h_bf6", [P, 2 * CHUNK * PACK], BF16, reuse=HALF * 2)
-        hidden(6)
-        gate_product(7)
-        hidden(7)
         second_product(1, 0)
-        quantise_h(6, 8)
-        pick_residual(3, 0, reuse=0)
-        combine(0, 0, scaled_reuse=HALF * 4)
+        h_w[1] = tile("h_w1", [P, HALF], U32)
+        quantise_h(4, 8)
+        pick_residual(3, 0, reuse=T * 4)
+        combine(0, 0, scaled_reuse=(T + HALF) * 4)
         place(0, 0)
-        combine(1, 0, scaled_reuse="total0_0")
+        combine(1, 0, total_reuse="total0_0")
         second_product(0, 1)
         combine(0, 1)
         second_product(1, 1)

@@ -221,6 +221,7 @@ def tile_list_modp_gsigm_res_kernel(
             )
 
         y = {}
+        y_whole = [tile("y%d" % n, [P, J], F32) for n in range(ROW_BLOCKS)]
 
         def second_product(n, half):
             cols = slice(half * HALF, (half + 1) * HALF)
@@ -234,10 +235,10 @@ def tile_list_modp_gsigm_res_kernel(
                 start=True,
                 stop=True,
             )
-            y[n, half] = tile("y%d_%d" % (n, half), [P, HALF], F32)
-            nc.scalar.copy(y[n, half][:], acc[:])
+            y[n, half] = y_whole[n][:, cols]
+            nc.scalar.copy(y[n, half], acc[:])
 
-        picked = {}
+        picked, picked_whole = {}, {}
 
         def pick_residual(n, half, reuse=None):
             picked[n, half] = tile("picked%d_%d" % (n, half), [P, HALF], F32, reuse=reuse)[:]
@@ -246,6 +247,7 @@ def tile_list_modp_gsigm_res_kernel(
         def pick_whole(n, reuse=None):
             whole = tile("picked%d" % n, [P, J], F32, reuse=reuse)
             nc.vector.tensor_copy(whole[:], res[n][:].indirect(offsets[:]))
+            picked_whole[n] = whole
             for half in range(2):
                 picked[n, half] = whole[:, half * HALF : (half + 1) * HALF]
 
@@ -253,7 +255,7 @@ def tile_list_modp_gsigm_res_kernel(
 
         def combine(n, half, total_reuse=None, scaled_reuse=None, into=None):
             total = tile("total%d_%d" % (n, half), [P, HALF], F32, reuse=total_reuse)
-            nc.gpsimd.tensor_tensor(total[:], picked[n, half], y[n, half][:], ADD)
+            nc.gpsimd.tensor_tensor(total[:], picked[n, half], y[n, half], ADD)
             if into is None:
                 scaled[n, half] = tile("scaled%d_%d" % (n, half), [P, HALF], F32, reuse=scaled_reuse)
                 into = scaled[n, half][:]
@@ -300,9 +302,13 @@ def tile_list_modp_gsigm_res_kernel(
         pick_residual(3, 1, reuse="scaled0_1")
         place(1, 1)
         for n in range(2, ROW_BLOCKS):
-            whole = tile("scaled%d" % n, [P, J], F32)
             for half in range(2):
                 second_product(n, half)
-                combine(n, half, into=whole[:, half * HALF : (half + 1) * HALF])
-            nc.vector.tensor_copy(pages[n % 2][:].indirect(offsets[:]), whole[:])
+            total = tile("total%d" % n, [P, J], F32)
+            if n in picked_whole:
+                nc.gpsimd.tensor_tensor(total[:], picked_whole[n][:], y_whole[n][:], ADD)
+            else:
+                for half in range(2):
+                    nc.gpsimd.tensor_tensor(total[:, half * HALF : (half + 1) * HALF], picked[n, half], y[n, half], ADD)
+            nc.vector.tensor_tensor(pages[n % 2][:].indirect(offsets[:]), total[:], weight[:], MULT)
             nc.sync.dma_start(out=out[n * P : (n + 1) * P, :], in_=pages[n % 2][:])

@@ -32,7 +32,6 @@ CHUNK = 128
 VECTOR_CHUNKS = (4, 5, 6, 7)
 TAB_SC_FIRST = QUAD - PASSES * SC_ROWS
 SC_SPAN = (QUADS - 1) * QUAD + SC_ROWS
-WU_PIECES = (((0, 256), (256, 512)), ((0, 256), (256, 384), (384, 512)))
 
 
 def tile_list_modp_gsigm_res_kernel(
@@ -56,7 +55,7 @@ def tile_list_modp_gsigm_res_kernel(
         def entries(j0, j1):
             return offsets[:, j0 // LIST_ROWS : j1 // LIST_ROWS]
 
-        wg_sc_raw = tile("wg_sc_raw", [P, PASSES * R], U8)
+        wg_sc_raw = tile("wg_sc_raw", [P, PASSES * R], U8, reuse=0)
         nc.gpsimd.memset(wg_sc_raw[:].bitcast(I32), 0)
         tab_sc = tile("tab_sc", [P, T], U8)
         for q in range(QUADS):
@@ -66,43 +65,39 @@ def tile_list_modp_gsigm_res_kernel(
                 in_=tab_scales[:, SC_ROWS * q : SC_ROWS * (q + 1), :].bitcast(I32),
             )
 
-        x_sc = [tile("x_sc%d" % a, [P, J], U8) for a in range(PASSES)]
-        for a in range(PASSES):
-            nc.gpsimd.memset(x_sc[a][:].bitcast(I32), 0)
-        pages = [tile("page0", [P, T], F32)]
-        nc.gpsimd.memset(pages[0][:], 0.0)
+        x_sc = tile("x_sc", [P, PASSES * J], U8)
+        nc.gpsimd.memset(x_sc[:].bitcast(I32), 0)
+        pages = [tile("page%d" % i, [P, T], F32) for i in range(2)]
+        for page in pages:
+            nc.gpsimd.memset(page[:], 0.0)
 
-        warm = tile("warm", [P, 1], F32)
-        nc.scalar.activation(warm[:], pages[0][:, 0:1], SIGMOID)
+        wu_raw = []
 
-        wu_raw = {}
-
-        def load_wu(a, r0, r1, reuse=None):
-            wu_raw[a, r0] = tile("wu_raw%d_%d" % (a, r0), [P, PACK, r1 - r0], F32, reuse=reuse)
-            rows = wu[K_PASS * a : K_PASS * (a + 1), r0:r1]
-            nc.sync.dma_start(out=wu_raw[a, r0][:], in_=rows.rearrange("(p i) r -> p i r", i=PACK))
+        def load_wu(a):
+            wu_raw.append(tile("wu_raw%d" % a, [P, PACK, R], F32))
+            rows = wu[K_PASS * a : K_PASS * (a + 1), :]
+            nc.sync.dma_start(out=wu_raw[a][:], in_=rows.rearrange("(p i) r -> p i r", i=PACK))
 
         tab_w = tile("tab_w", [P, T], I32)
         nc.sync.dma_start(out=tab_w[:], in_=tab_words[0].rearrange("p t b -> p (t b)").bitcast(I32))
         wg_w_raw = tile("wg_w_raw", [P, PASSES, FP4_BYTES * R], U8)
         nc.sync.dma_start(out=wg_w_raw[:].bitcast(I32), in_=wg_words.rearrange("a p b -> p a b").bitcast(I32))
-        load_wu(0, *WU_PIECES[0][0])
         for q in range(QUADS):
             rows = wg_sc_raw[QUAD * q : QUAD * q + SC_ROWS, :]
             nc.sync.dma_start(
                 out=rows.rearrange("p (a r) -> p a r", a=PASSES).bitcast(I32),
                 in_=wg_scales[:, SC_ROWS * q : SC_ROWS * (q + 1), :].rearrange("a q r -> q a r").bitcast(I32),
             )
-        load_wu(0, *WU_PIECES[0][1], reuse=0)
-        for r0, r1 in WU_PIECES[1]:
-            load_wu(1, r0, r1)
+        for a in range(PASSES):
+            load_wu(a)
 
         picked_sc = tile("picked_sc", [P, J], U8)
         nc.vector.tensor_copy(picked_sc[:], tab_sc[:].indirect(offsets[:]))
         for a in range(PASSES):
             first = TAB_SC_FIRST + SC_ROWS * a
             nc.sync.dma_start(
-                out=x_sc[a][0:SC_SPAN, :].bitcast(I32), in_=picked_sc[first : first + SC_SPAN, :].bitcast(I32)
+                out=x_sc[0:SC_SPAN, a * J : (a + 1) * J].bitcast(I32),
+                in_=picked_sc[first : first + SC_SPAN, :].bitcast(I32),
             )
 
         both = tile("both", [P, J], U32)
@@ -128,17 +123,16 @@ def tile_list_modp_gsigm_res_kernel(
         for a in range(PASSES):
             wu_bf = tile("wu_bf%d" % a, [P, PACK * R], BF16)
             by_slot = wu_bf[:].rearrange("p (t m i) -> p m t i", t=PACK, i=PACK)
-            for r0, r1 in WU_PIECES[a]:
-                nc.scalar.copy(
-                    by_slot[:, r0 // PACK : r1 // PACK], wu_raw[a, r0][:].rearrange("p i (m t) -> p m t i", t=PACK)
-                )
+            source = wu_raw[a][:].rearrange("p i (m t) -> p m t i", t=PACK)
+            if a < PASSES - 1:
+                nc.scalar.copy(by_slot, source)
+            else:
+                nc.scalar.copy(by_slot[:, : P // 2], source[:, : P // 2])
+                nc.vector.tensor_copy(by_slot[:, P // 2 :], source[:, P // 2 :])
             wu_w.append(tile("wu_w%d" % a, [P, R], U32))
             wu_sc.append(tile("wu_sc%d" % a, [P, R], U8))
             nc.vector.quantize_mx(out=wu_w[a][:].bitcast(FP8X4), scales=wu_sc[a][:], in_=wu_bf[:])
 
-
-        pages.append(tile("page1", [P, T], F32, reuse="wu_bf1"))
-        nc.gpsimd.memset(pages[1][:], 0.0)
 
         res = []
 
@@ -147,18 +141,18 @@ def tile_list_modp_gsigm_res_kernel(
             nc.sync.dma_start(out=res[n][:], in_=rT[n * P : (n + 1) * P, :])
 
         load_res(0, "tab_sc")
-        load_res(1, "wu_raw0_0")
+        load_res(1, "both")
         load_res(2, 0)
-        wd_w = tile("wd_w", [P, FP4_BYTES * N], U8, reuse="wu_raw1_0")
+        wd_w = tile("wd_w", [P, FP4_BYTES * N], U8, reuse="wu_raw0")
         nc.sync.dma_start(out=wd_w[:].bitcast(I32), in_=wd_words[0].bitcast(I32))
-        wd_sc = tile("wd_sc", [P, N], U8, reuse="wu_raw1_256")
+        wd_sc = tile("wd_sc", [P, N], U8, reuse="wu_bf0")
         nc.gpsimd.memset(wd_sc[:].bitcast(I32), 0)
         for q in range(QUADS):
             nc.sync.dma_start(
                 out=wd_sc[QUAD * q : QUAD * q + SC_ROWS, :].bitcast(I32),
                 in_=wd_scales[0, SC_ROWS * q : SC_ROWS * (q + 1), :].bitcast(I32),
             )
-        weight = tile("weight", [P, J], F32, reuse="wu_raw1_384")
+        weight = tile("weight", [P, J], F32, reuse="wu_raw1")
         nc.sync.dma_start(out=weight[:], in_=wgo)
 
         def first_product(bank, c, words, scales):
@@ -170,7 +164,7 @@ def tile_list_modp_gsigm_res_kernel(
                         lhsT=words(a, t),
                         lhsT_scale=scales(a, t),
                         rhs=x_w[:, b0 : b0 + FP4_BYTES * CHUNK].bitcast(FP4X4),
-                        rhs_scale=x_sc[a][:, c * CHUNK : (c + 1) * CHUNK],
+                        rhs_scale=x_sc[:, a * J + c * CHUNK : a * J + (c + 1) * CHUNK],
                         start=(a == 0 and t == 0),
                         stop=(a == PASSES - 1 and t == PACK - 1),
                     )

@@ -29,7 +29,7 @@ LIST_ROWS = 16
 ROW_BLOCKS = N // P
 HALF = J // 2
 CHUNK = 128
-VECTOR_CHUNKS = (4, 5, 6, 7)
+VECTOR_CHUNKS = (5, 6, 7)
 TAB_SC_FIRST = QUAD - PASSES * SC_ROWS
 SC_SPAN = (QUADS - 1) * QUAD + SC_ROWS
 
@@ -262,11 +262,11 @@ def tile_list_modp_gsigm_res_kernel(
                 nc.sync.dma_start(out=out[n * P : (n + 1) * P, :], in_=page[:])
 
         gate_product(0)
-        gate_product(1)
         pick_whole(0)
         load_res(3, "tab_sc")
         h_bf[0] = tile("h_bf0", [P, HALF * PACK], BF16, reuse=T * 4)
         hidden(0)
+        gate_product(1)
         hidden(1)
         pick_whole(1)
         for c in (2, 3):
@@ -280,29 +280,20 @@ def tile_list_modp_gsigm_res_kernel(
             gate_product(c)
             hidden(c)
         second_product(0, 0)
-        second_product(1, 0)
         h_w[1] = tile("h_w1", [P, HALF], U32)
         quantise_h(4, 8)
-        pick_residual(3, 0, reuse=T * 4)
-        combine(0, 0, scaled_reuse=(T + HALF) * 4)
+        pick_whole(3, reuse=3 * HALF * 4)
+        combine(0, 0, total_reuse=(T + HALF) * 4)
         place(0, 0)
-        combine(1, 0, total_reuse="total0_0")
-        second_product(0, 1)
-        combine(0, 1)
-        second_product(1, 1)
-        combine(1, 1)
-        place(1, 0)
-        place(0, 1)
-        pick_residual(3, 1, reuse="scaled0_1")
-        place(1, 1)
+        chain = (T + 2 * HALF) * 4
+        for n, half in ((0, 1), (1, 0), (1, 1)):
+            second_product(n, half)
+            combine(n, half, total_reuse=chain + 3 * HALF * 2)
+            place(n, half)
         for n in range(2, ROW_BLOCKS):
             for half in range(2):
                 second_product(n, half)
-            total = tile("total%d" % n, [P, J], F32)
-            if n in picked_whole:
-                nc.gpsimd.tensor_tensor(total[:], picked_whole[n][:], y_whole[n][:], ADD)
-            else:
-                for half in range(2):
-                    nc.gpsimd.tensor_tensor(total[:, half * HALF : (half + 1) * HALF], picked[n, half], y[n, half], ADD)
+            total = tile("total%d" % n, [P, J], F32, reuse=chain + (n - 2) * J * 4)
+            nc.gpsimd.tensor_tensor(total[:], picked_whole[n][:], y_whole[n][:], ADD)
             nc.vector.tensor_tensor(pages[n % 2][:].indirect(offsets[:]), total[:], weight[:], MULT)
             nc.sync.dma_start(out=out[n * P : (n + 1) * P, :], in_=pages[n % 2][:])

@@ -1,6 +1,7 @@
 from contextlib import ExitStack
 
 import concourse.mybir as mybir
+from concourse.masks import make_identity
 
 K, R, N, T, J = 1024, 512, 512, 2048, 1024
 FLOPS = 2 * (2 * K * R * J + R * N * J)
@@ -14,8 +15,8 @@ U8 = mybir.dt.uint8
 FP8X4 = mybir.dt.float8_e4m3fn_x4
 FP4X4 = mybir.dt.float4_e2m1fn_x4
 MULT = mybir.AluOpType.mult
-ADD = mybir.AluOpType.add
 SIGMOID = mybir.ActivationFunctionType.Sigmoid
+COPY = mybir.ActivationFunctionType.Copy
 
 P = 128
 PACK = 4
@@ -29,7 +30,9 @@ LIST_ROWS = 16
 ROW_BLOCKS = N // P
 HALF = J // 2
 CHUNK = 128
-VECTOR_CHUNKS = (5, 6, 7)
+CHUNKS = J // CHUNK
+BANK_BYTES = 2048
+PER_HALF = HALF // CHUNK
 TAB_SC_FIRST = QUAD - PASSES * SC_ROWS
 SC_SPAN = (QUADS - 1) * QUAD + SC_ROWS
 
@@ -67,8 +70,13 @@ def tile_list_modp_gsigm_res_kernel(
 
         x_sc = tile("x_sc", [P, PASSES * J], U8)
         nc.gpsimd.memset(x_sc[:].bitcast(I32), 0)
-        pages = [tile("page%d" % i, [P, T], F32) for i in range(2)]
-        for page in pages:
+        weight_rows = tile("weight_rows", [P, CHUNK], F32)
+        nc.gpsimd.memset(weight_rows[:], 0.0)
+        identity = tile("identity", [P, P], F32)
+        make_identity(nc, identity[:])
+        pages = [tile("page%d" % i, [P, T], F32) for i in range(3)]
+        nc.vector.memset(pages[0][:], 0.0)
+        for page in pages[1:]:
             nc.gpsimd.memset(page[:], 0.0)
 
         wu_raw = []
@@ -152,8 +160,7 @@ def tile_list_modp_gsigm_res_kernel(
                 out=wd_sc[QUAD * q : QUAD * q + SC_ROWS, :].bitcast(I32),
                 in_=wd_scales[0, SC_ROWS * q : SC_ROWS * (q + 1), :].bitcast(I32),
             )
-        weight = tile("weight", [P, J], F32, reuse="wu_raw1")
-        nc.sync.dma_start(out=weight[:], in_=wgo)
+        nc.sync.dma_start(out=weight_rows[0:CHUNKS, :], in_=wgo[0:1, :].rearrange("o (c j) -> (o c) j", c=CHUNKS))
 
         def first_product(bank, c, words, scales):
             for a in range(PASSES):
@@ -172,128 +179,178 @@ def tile_list_modp_gsigm_res_kernel(
         h_w, h_bf = {}, {}
         h_sc = tile("h_sc", [P, J], U8)
 
-        def bank(shape):
-            return psum.tile(shape, F32, name="bank", tag="bank", bufs=8)
+        def bank(name, shape, number):
+            return psum.tile(shape, F32, name=name, offset=number * BANK_BYTES)
 
-        gate = {}
+        gate, sums = {}, {}
 
-        def gate_product(c):
-            ga = bank([P, PACK, CHUNK])
-            first_product(
-                ga,
-                c,
-                lambda a, t: wg_w[:, FP4_BYTES * (a * R + t * P) : FP4_BYTES * (a * R + (t + 1) * P)].bitcast(FP4X4),
-                lambda a, t: wg_sc[:, a * R + t * P : a * R + (t + 1) * P],
-            )
-            gate[c] = tile("gate%d" % c, [P, CHUNK, PACK], F32)
-            nc.scalar.activation(gate[c][:], ga[:].rearrange("p t j -> p j t"), SIGMOID)
+        def multiply(kind, c, number):
+            sums[kind, c] = bank("%s%d" % (kind, c), [P, PACK, CHUNK], number)
+            if kind == "ga":
+                first_product(
+                    sums[kind, c],
+                    c,
+                    lambda a, t: wg_w[:, FP4_BYTES * (a * R + t * P) : FP4_BYTES * (a * R + (t + 1) * P)].bitcast(FP4X4),
+                    lambda a, t: wg_sc[:, a * R + t * P : a * R + (t + 1) * P],
+                )
+            else:
+                first_product(
+                    sums[kind, c],
+                    c,
+                    lambda a, t: wu_w[a][:, t * P : (t + 1) * P].bitcast(FP8X4),
+                    lambda a, t: wu_sc[a][:, t * P : (t + 1) * P],
+                )
+
+        def squash(c, reuse=None):
+            gate[c] = tile("gate%d" % c, [P, CHUNK, PACK], F32, reuse=reuse)
+            nc.scalar.activation(gate[c][:], sums["ga", c][:].rearrange("p t j -> p j t"), SIGMOID)
 
         def hidden(c, reuse=None):
-            ub = bank([P, PACK, CHUNK])
-            first_product(
-                ub,
-                c,
-                lambda a, t: wu_w[a][:, t * P : (t + 1) * P].bitcast(FP8X4),
-                lambda a, t: wu_sc[a][:, t * P : (t + 1) * P],
-            )
-            first = max(c0 for c0 in h_bf if c0 <= c)
-            j0 = (c - first) * CHUNK
-            h = h_bf[first][:, j0 * PACK : (j0 + CHUNK) * PACK].rearrange("p (j t) -> p j t", t=PACK)
-            if c in VECTOR_CHUNKS:
-                nc.vector.tensor_tensor(h, ub[:].rearrange("p t j -> p j t"), gate[c][:], MULT)
-            else:
-                up = tile("up%d" % c, [P, CHUNK, PACK], F32, reuse=reuse)
-                nc.scalar.copy(up[:], ub[:].rearrange("p t j -> p j t"))
-                nc.gpsimd.tensor_tensor(h, up[:], gate[c][:], MULT)
+            half, j0 = divmod(c * CHUNK, HALF)
+            h = h_bf[half][:, j0 * PACK : (j0 + CHUNK) * PACK].rearrange("p (j t) -> p j t", t=PACK)
+            up = tile("up%d" % c, [P, CHUNK, PACK], F32, reuse=reuse)
+            nc.scalar.copy(up[:], sums["ub", c][:].rearrange("p t j -> p j t"))
+            nc.gpsimd.tensor_tensor(h, up[:], gate[c][:], MULT)
 
-        def quantise_h(c0, c1):
-            half, j0 = divmod(c0 * CHUNK, HALF)
+        def first_bank(c):
+            return 2 * (c % 3) if c < 6 else 2 * (c - 6)
+
+        def gate_stage(c):
+            multiply("ga", c, first_bank(c))
+            if c < CHUNKS - 1:
+                squash(c)
+
+        def up_stage(c):
+            multiply("ub", c, first_bank(c) + 1)
+            if c < CHUNKS - 2:
+                hidden(c)
+
+        def quantise_h(half):
             nc.vector.quantize_mx(
-                out=h_w[half][:, j0 : j0 + (c1 - c0) * CHUNK].bitcast(FP8X4),
-                scales=h_sc[:, c0 * CHUNK : c1 * CHUNK],
-                in_=h_bf[c0][:],
+                out=h_w[half][:].bitcast(FP8X4), scales=h_sc[:, half * HALF : (half + 1) * HALF], in_=h_bf[half][:]
             )
 
-        y = {}
-        y_whole = [tile("y%d" % n, [P, J], F32) for n in range(ROW_BLOCKS)]
+        weight = tile("weight", [P, CHUNKS], F32)
 
-        def second_product(n, half):
-            cols = slice(half * HALF, (half + 1) * HALF)
-            acc = bank([P, HALF])
+        def turn_weight():
+            turned = bank("weight_turned", [P, P], 7)
+            nc.tensor.transpose(turned[:], weight_rows[:], identity[:])
+            nc.scalar.copy(weight[:], turned[:, 0:CHUNKS])
+
+        picked = {}
+
+        def pick(n, reuse=None):
+            picked[n] = tile("picked%d" % n, [P, J], F32, reuse=reuse)
+            nc.vector.tensor_copy(picked[n][:], res[n][:].indirect(offsets[:]))
+
+        terms, total = {}, {}
+
+        def turn_residual(into, n, c):
+            nc.tensor.transpose(into, picked[n][:, c * CHUNK : (c + 1) * CHUNK], identity[:])
+
+        def second_product(into, n, c):
+            half, j0 = divmod(c * CHUNK, HALF)
             nc.tensor.matmul_mx(
-                out=acc[:],
-                lhsT=wd_w[:, FP4_BYTES * n * P : FP4_BYTES * (n + 1) * P].bitcast(FP4X4),
-                lhsT_scale=wd_sc[:, n * P : (n + 1) * P],
-                rhs=h_w[half][:].bitcast(FP8X4),
-                rhs_scale=h_sc[:, cols],
+                out=into,
+                lhsT=h_w[half][:, j0 : j0 + CHUNK].bitcast(FP8X4),
+                lhsT_scale=h_sc[:, c * CHUNK : (c + 1) * CHUNK],
+                rhs=wd_w[:, FP4_BYTES * n * P : FP4_BYTES * (n + 1) * P].bitcast(FP4X4),
+                rhs_scale=wd_sc[:, n * P : (n + 1) * P],
                 start=True,
                 stop=True,
             )
-            y[n, half] = y_whole[n][:, cols]
-            nc.scalar.copy(y[n, half], acc[:])
 
-        picked, picked_whole = {}, {}
+        def terms_tile(n, c):
+            reuse = last_terms_at if (n, c) == (0, PER_HALF - 1) else "terms%d_%d" % (n, c % PER_HALF)
+            terms[n, c] = tile("terms%d_%d" % (n, c), [P, 2, P], F32, reuse=reuse)
 
-        def pick_residual(n, half, reuse=None):
-            picked[n, half] = tile("picked%d_%d" % (n, half), [P, HALF], F32, reuse=reuse)[:]
-            nc.vector.tensor_copy(picked[n, half], res[n][:].indirect(entries(half * HALF, (half + 1) * HALF)))
+        def weigh(n, c0, number):
+            both_terms = bank("terms%d_%d" % (n, c0), [P, 2, 2, P], number)
+            for c in (c0, c0 + 1):
+                turn_residual(both_terms[:, c - c0, 0, :], n, c)
+            for c in (c0, c0 + 1):
+                second_product(both_terms[:, c - c0, 1, :], n, c)
+            for c in (c0, c0 + 1):
+                terms_tile(n, c)
+                nc.scalar.activation(terms[n, c][:], both_terms[:, c - c0], COPY, scale=weight[:, c : c + 1])
 
-        def pick_whole(n, reuse=None):
-            whole = tile("picked%d" % n, [P, J], F32, reuse=reuse)
-            nc.vector.tensor_copy(whole[:], res[n][:].indirect(offsets[:]))
-            picked_whole[n] = whole
-            for half in range(2):
-                picked[n, half] = whole[:, half * HALF : (half + 1) * HALF]
+        def weigh_first(k, make, number):
+            one_term = bank("first_term%d" % k, [P, PER_HALF, P], number)
+            for c in range(PER_HALF):
+                make(one_term[:, c, :], 0, c)
+            for c in range(PER_HALF):
+                if k == 0:
+                    terms_tile(0, c)
+                nc.scalar.activation(terms[0, c][:, k, :], one_term[:, c, :], COPY, scale=weight[:, c : c + 1])
 
-        scaled = {}
+        def combine(n, half, number, reuse=None):
+            acc = bank("sum%d_%d" % (n, half), [P, PER_HALF, CHUNK], number)
+            for i in range(PER_HALF):
+                for k in range(2):
+                    term = terms[n, half * PER_HALF + i][:, k, :]
+                    nc.tensor.matmul(acc[:, i, :], term, identity[:], start=(k == 0), stop=(k == 1), is_transpose=True)
+            if (n, half) not in total:
+                total[n, half] = tile("total%d_%d" % (n, half), [P, HALF], F32, reuse=reuse)[:]
+            nc.scalar.copy(total[n, half], acc[:].rearrange("p i j -> p (i j)"))
 
-        def combine(n, half, total_reuse=None, scaled_reuse=None, into=None):
-            total = tile("total%d_%d" % (n, half), [P, HALF], F32, reuse=total_reuse)
-            nc.gpsimd.tensor_tensor(total[:], picked[n, half], y[n, half], ADD)
-            if into is None:
-                scaled[n, half] = tile("scaled%d_%d" % (n, half), [P, HALF], F32, reuse=scaled_reuse)
-                into = scaled[n, half][:]
-            nc.gpsimd.tensor_tensor(into, total[:], weight[:, half * HALF : (half + 1) * HALF], MULT)
+        def unit(n, half, numbers):
+            weigh(n, half * PER_HALF, numbers[0])
+            weigh(n, half * PER_HALF + 2, numbers[1])
+            combine(n, half, numbers[2])
+
+        def store(n):
+            nc.sync.dma_start(out=out[n * P : (n + 1) * P, :], in_=pages[n % len(pages)][:])
 
         def place(n, half):
-            page = pages[n % 2]
-            nc.vector.tensor_copy(page[:].indirect(entries(half * HALF, (half + 1) * HALF)), scaled[n, half][:])
+            page = pages[n % len(pages)]
+            nc.vector.tensor_copy(page[:].indirect(entries(half * HALF, (half + 1) * HALF)), total[n, half])
             if half == 1:
-                nc.sync.dma_start(out=out[n * P : (n + 1) * P, :], in_=page[:])
+                store(n)
 
-        gate_product(0)
-        pick_whole(0)
-        load_res(3, "tab_sc")
-        h_bf[0] = tile("h_bf0", [P, HALF * PACK], BF16, reuse=T * 4)
-        hidden(0)
-        gate_product(1)
-        hidden(1)
-        pick_whole(1)
-        for c in (2, 3):
-            gate_product(c)
-            hidden(c)
-        pick_whole(2)
+        h_at = T * 4
+        first_at = h_at + 2 * HALF * PACK * 2
+        turn_weight()
+        last_terms_at = first_at + 2 * HALF * 4
+        load_res(3, "wu_raw1")
+        gate_stage(0)
+        pick(0)
+        h_bf[0] = tile("h_bf0", [P, HALF * PACK], BF16, reuse=h_at)
+        for c in range(PER_HALF):
+            gate_stage(c + 1)
+            up_stage(c)
+            if c == 1:
+                pick(1)
+        pick(2)
         h_w[0] = tile("h_w0", [P, HALF], U32, reuse=0)
-        quantise_h(0, 4)
-        h_bf[4] = tile("h_bf4", [P, HALF * PACK], BF16, reuse=T * 4)
-        for c in (4, 5, 6, 7):
-            gate_product(c)
-            hidden(c)
-        second_product(0, 0)
-        h_w[1] = tile("h_w1", [P, HALF], U32)
-        quantise_h(4, 8)
-        pick_whole(3, reuse=3 * HALF * 4)
-        combine(0, 0, total_reuse=(T + HALF) * 4)
+        quantise_h(0)
+        pick(3, reuse=h_at + 64 - J * 4)
+        h_bf[1] = tile("h_bf1", [P, HALF * PACK], BF16, reuse=h_at + HALF * PACK * 2 - 64)
+        gate_stage(5)
+        up_stage(4)
+        weigh_first(0, turn_residual, 6)
+        gate_stage(6)
+        up_stage(5)
+        up_stage(6)
+        gate_stage(7)
+        up_stage(7)
+        weigh_first(1, second_product, 7)
+        combine(0, 0, 4, reuse=first_at)
         place(0, 0)
-        chain = (T + 2 * HALF) * 4
-        for n, half in ((0, 1), (1, 0), (1, 1)):
-            second_product(n, half)
-            combine(n, half, total_reuse=chain + 3 * HALF * 2)
-            place(n, half)
-        for n in range(2, ROW_BLOCKS):
-            for half in range(2):
-                second_product(n, half)
-            total = tile("total%d" % n, [P, J], F32, reuse=chain + (n - 2) * J * 4)
-            nc.gpsimd.tensor_tensor(total[:], picked_whole[n][:], y_whole[n][:], ADD)
-            nc.vector.tensor_tensor(pages[n % 2][:].indirect(offsets[:]), total[:], weight[:], MULT)
-            nc.sync.dma_start(out=out[n * P : (n + 1) * P, :], in_=pages[n % 2][:])
+        hidden(6, reuse="terms0_0")
+        squash(7, reuse=last_terms_at + 64 - CHUNK * PACK * 4)
+        hidden(7, reuse=last_terms_at + 2 * P * 4 - 64)
+        h_w[1] = tile("h_w1", [P, HALF], U32, reuse=first_at)
+        quantise_h(1)
+        unit(1, 0, (2, 3, 5))
+        place(1, 0)
+        unit(2, 0, (3, 5, 6))
+        place(2, 0)
+        for n in range(3):
+            unit(n, 1, (0, 1, 2) if n % 2 == 0 else (3, 4, 5))
+            place(n, 1)
+        last = tile("total_last", [P, J], F32)
+        for half in range(2):
+            total[3, half] = last[:, half * HALF : (half + 1) * HALF]
+            unit(3, half, (0, 1, 2) if half else (6, 7, 3))
+        nc.vector.tensor_copy(pages[0][:].indirect(offsets[:]), last[:])
+        store(3)

@@ -1,7 +1,6 @@
 from contextlib import ExitStack
 
 import concourse.mybir as mybir
-from concourse.masks import make_identity
 
 K, R, N, T, J = 1024, 512, 512, 2048, 1024
 FLOPS = 2 * (2 * K * R * J + R * N * J)
@@ -15,8 +14,8 @@ U8 = mybir.dt.uint8
 FP8X4 = mybir.dt.float8_e4m3fn_x4
 FP4X4 = mybir.dt.float4_e2m1fn_x4
 MULT = mybir.AluOpType.mult
+ADD = mybir.AluOpType.add
 SIGMOID = mybir.ActivationFunctionType.Sigmoid
-COPY = mybir.ActivationFunctionType.Copy
 
 P = 128
 PACK = 4
@@ -31,10 +30,10 @@ ROW_BLOCKS = N // P
 HALF = J // 2
 CHUNK = 128
 CHUNKS = J // CHUNK
+VECTOR_CHUNKS = (5, 6, 7)
 BANK_BYTES = 2048
 PER_HALF = HALF // CHUNK
-TAB_SC_FIRST = QUAD - PASSES * SC_ROWS
-SC_SPAN = (QUADS - 1) * QUAD + SC_ROWS
+TAB_SC_FIRST = QUAD // 2
 
 
 def tile_list_modp_gsigm_res_kernel(
@@ -61,20 +60,14 @@ def tile_list_modp_gsigm_res_kernel(
         wg_sc_raw = tile("wg_sc_raw", [P, PASSES * R], U8, reuse=0)
         nc.gpsimd.memset(wg_sc_raw[:].bitcast(I32), 0)
         tab_sc = tile("tab_sc", [P, T], U8)
-        for q in range(QUADS):
-            nc.gpsimd.memset(tab_sc[QUAD * q : QUAD * q + TAB_SC_FIRST, :].bitcast(I32), 0)
-            nc.sync.dma_start(
-                out=tab_sc[QUAD * q + TAB_SC_FIRST : QUAD * (q + 1), :].bitcast(I32),
-                in_=tab_scales[:, SC_ROWS * q : SC_ROWS * (q + 1), :].bitcast(I32),
-            )
+        rows = tab_scales.rearrange("a (h o r) t -> o (a h) r t", h=2, o=2).bitcast(I32)
+        for odd in range(2):
+            nc.gpsimd.memset(tab_sc[QUAD * odd : QUAD * odd + TAB_SC_FIRST, :].bitcast(I32), 0)
+            nc.sync.dma_start(out=tab_sc[QUAD * odd + TAB_SC_FIRST : QUAD * (odd + 1), :].bitcast(I32), in_=rows[odd])
+        nc.gpsimd.memset(tab_sc[P // 2 :, :].bitcast(I32), 0)
 
         x_sc = tile("x_sc", [P, PASSES * J], U8)
-        nc.gpsimd.memset(x_sc[:].bitcast(I32), 0)
-        weight_rows = tile("weight_rows", [P, CHUNK], F32)
-        nc.gpsimd.memset(weight_rows[:], 0.0)
-        identity = tile("identity", [P, P], F32)
-        make_identity(nc, identity[:])
-        pages = [tile("page%d" % i, [P, T], F32) for i in range(3)]
+        pages = [tile("page%d" % i, [P, T], F32) for i in range(2)]
         nc.vector.memset(pages[0][:], 0.0)
         for page in pages[1:]:
             nc.gpsimd.memset(page[:], 0.0)
@@ -102,11 +95,12 @@ def tile_list_modp_gsigm_res_kernel(
         picked_sc = tile("picked_sc", [P, J], U8)
         nc.vector.tensor_copy(picked_sc[:], tab_sc[:].indirect(offsets[:]))
         for a in range(PASSES):
-            first = TAB_SC_FIRST + SC_ROWS * a
-            nc.sync.dma_start(
-                out=x_sc[0:SC_SPAN, a * J : (a + 1) * J].bitcast(I32),
-                in_=picked_sc[first : first + SC_SPAN, :].bitcast(I32),
-            )
+            for upper in range(2):
+                first = TAB_SC_FIRST + SC_ROWS * (2 * a + upper)
+                nc.sync.dma_start(
+                    out=x_sc[P // 2 * upper : P // 2 * (upper + 1), a * J : (a + 1) * J].bitcast(I32),
+                    in_=picked_sc[first : first + P // 2, :].bitcast(I32),
+                )
 
         both = tile("both", [P, J], U32)
         nc.vector.tensor_copy(both[:], tab_w[:].bitcast(U32).indirect(offsets[:]))
@@ -160,7 +154,6 @@ def tile_list_modp_gsigm_res_kernel(
                 out=wd_sc[QUAD * q : QUAD * q + SC_ROWS, :].bitcast(I32),
                 in_=wd_scales[0, SC_ROWS * q : SC_ROWS * (q + 1), :].bitcast(I32),
             )
-        nc.sync.dma_start(out=weight_rows[0:CHUNKS, :], in_=wgo[0:1, :].rearrange("o (c j) -> (o c) j", c=CHUNKS))
 
         def first_product(bank, c, words, scales):
             for a in range(PASSES):
@@ -208,34 +201,21 @@ def tile_list_modp_gsigm_res_kernel(
         def hidden(c, reuse=None):
             half, j0 = divmod(c * CHUNK, HALF)
             h = h_bf[half][:, j0 * PACK : (j0 + CHUNK) * PACK].rearrange("p (j t) -> p j t", t=PACK)
-            up = tile("up%d" % c, [P, CHUNK, PACK], F32, reuse=reuse)
-            nc.scalar.copy(up[:], sums["ub", c][:].rearrange("p t j -> p j t"))
-            nc.gpsimd.tensor_tensor(h, up[:], gate[c][:], MULT)
+            ub = sums["ub", c][:].rearrange("p t j -> p j t")
+            if c in VECTOR_CHUNKS:
+                nc.vector.tensor_tensor(h, ub, gate[c][:], MULT)
+            else:
+                up = tile("up%d" % c, [P, CHUNK, PACK], F32, reuse=reuse)
+                nc.scalar.copy(up[:], ub)
+                nc.gpsimd.tensor_tensor(h, up[:], gate[c][:], MULT)
 
-        def first_bank(c):
-            return 2 * (c % 3) if c < 6 else 2 * (c - 6)
-
-        def gate_stage(c):
-            multiply("ga", c, first_bank(c))
-            if c < CHUNKS - 1:
-                squash(c)
-
-        def up_stage(c):
-            multiply("ub", c, first_bank(c) + 1)
-            if c < CHUNKS - 2:
-                hidden(c)
+        GATE_BANKS = (0, 1, 2, 1, 0, 1, 0, 2)
+        UP_BANKS = (1, 2, 0, 3, 2, 3, 4, 5)
 
         def quantise_h(half):
             nc.vector.quantize_mx(
                 out=h_w[half][:].bitcast(FP8X4), scales=h_sc[:, half * HALF : (half + 1) * HALF], in_=h_bf[half][:]
             )
-
-        weight = tile("weight", [P, CHUNKS], F32)
-
-        def turn_weight():
-            turned = bank("weight_turned", [P, P], 7)
-            nc.tensor.transpose(turned[:], weight_rows[:], identity[:])
-            nc.scalar.copy(weight[:], turned[:, 0:CHUNKS])
 
         picked = {}
 
@@ -243,114 +223,91 @@ def tile_list_modp_gsigm_res_kernel(
             picked[n] = tile("picked%d" % n, [P, J], F32, reuse=reuse)
             nc.vector.tensor_copy(picked[n][:], res[n][:].indirect(offsets[:]))
 
-        terms, total = {}, {}
+        y, total = {}, {}
+        y_whole = [tile("y%d" % n, [P, J], F32) for n in range(ROW_BLOCKS)]
 
-        def turn_residual(into, n, c):
-            nc.tensor.transpose(into, picked[n][:, c * CHUNK : (c + 1) * CHUNK], identity[:])
-
-        def second_product(into, n, c):
-            half, j0 = divmod(c * CHUNK, HALF)
+        def second_product(n, half, number):
+            acc = bank("y%d_%d" % (n, half), [P, HALF], number)
             nc.tensor.matmul_mx(
-                out=into,
-                lhsT=h_w[half][:, j0 : j0 + CHUNK].bitcast(FP8X4),
-                lhsT_scale=h_sc[:, c * CHUNK : (c + 1) * CHUNK],
-                rhs=wd_w[:, FP4_BYTES * n * P : FP4_BYTES * (n + 1) * P].bitcast(FP4X4),
-                rhs_scale=wd_sc[:, n * P : (n + 1) * P],
+                out=acc[:],
+                lhsT=wd_w[:, FP4_BYTES * n * P : FP4_BYTES * (n + 1) * P].bitcast(FP4X4),
+                lhsT_scale=wd_sc[:, n * P : (n + 1) * P],
+                rhs=h_w[half][:].bitcast(FP8X4),
+                rhs_scale=h_sc[:, half * HALF : (half + 1) * HALF],
                 start=True,
                 stop=True,
             )
+            y[n, half] = y_whole[n][:, half * HALF : (half + 1) * HALF]
+            nc.scalar.copy(y[n, half], acc[:])
 
-        def terms_tile(n, c):
-            reuse = last_terms_at if (n, c) == (0, PER_HALF - 1) else "terms%d_%d" % (n, c % PER_HALF)
-            terms[n, c] = tile("terms%d_%d" % (n, c), [P, 2, P], F32, reuse=reuse)
-
-        def weigh(n, c0, number):
-            both_terms = bank("terms%d_%d" % (n, c0), [P, 2, 2, P], number)
-            for c in (c0, c0 + 1):
-                turn_residual(both_terms[:, c - c0, 0, :], n, c)
-            for c in (c0, c0 + 1):
-                second_product(both_terms[:, c - c0, 1, :], n, c)
-            for c in (c0, c0 + 1):
-                terms_tile(n, c)
-                nc.scalar.activation(terms[n, c][:], both_terms[:, c - c0], COPY, scale=weight[:, c : c + 1])
-
-        def weigh_first(k, make, number):
-            one_term = bank("first_term%d" % k, [P, PER_HALF, P], number)
-            for c in range(PER_HALF):
-                make(one_term[:, c, :], 0, c)
-            for c in range(PER_HALF):
-                if k == 0:
-                    terms_tile(0, c)
-                nc.scalar.activation(terms[0, c][:, k, :], one_term[:, c, :], COPY, scale=weight[:, c : c + 1])
-
-        def combine(n, half, number, reuse=None):
-            acc = bank("sum%d_%d" % (n, half), [P, PER_HALF, CHUNK], number)
-            for i in range(PER_HALF):
-                for k in range(2):
-                    term = terms[n, half * PER_HALF + i][:, k, :]
-                    nc.tensor.matmul(acc[:, i, :], term, identity[:], start=(k == 0), stop=(k == 1), is_transpose=True)
-            if (n, half) not in total:
+        def add_residual(n, half, reuse=None):
+            cols = slice(half * HALF, (half + 1) * HALF)
+            if n < 2:
                 total[n, half] = tile("total%d_%d" % (n, half), [P, HALF], F32, reuse=reuse)[:]
-            nc.scalar.copy(total[n, half], acc[:].rearrange("p i j -> p (i j)"))
+            else:
+                if half == 0:
+                    total[n] = tile("total%d" % n, [P, J], F32, reuse=reuse)
+                total[n, half] = total[n][:, cols]
+            nc.gpsimd.tensor_tensor(total[n, half], picked[n][:, cols], y[n, half], ADD)
 
-        def unit(n, half, numbers):
-            weigh(n, half * PER_HALF, numbers[0])
-            weigh(n, half * PER_HALF + 2, numbers[1])
-            combine(n, half, numbers[2])
+        def weigh_and_place(n, half, reuse=None):
+            cols = slice(half * HALF, (half + 1) * HALF)
+            scaled = tile("scaled%d_%d" % (n, half), [P, HALF], F32, reuse=reuse)
+            nc.gpsimd.tensor_tensor(scaled[:], total[n, half], weight[:, cols], MULT)
+            nc.vector.tensor_copy(pages[n][:].indirect(entries(half * HALF, (half + 1) * HALF)), scaled[:])
+            if half == 1:
+                store(n)
 
         def store(n):
             nc.sync.dma_start(out=out[n * P : (n + 1) * P, :], in_=pages[n % len(pages)][:])
 
-        def place(n, half):
-            page = pages[n % len(pages)]
-            nc.vector.tensor_copy(page[:].indirect(entries(half * HALF, (half + 1) * HALF)), total[n, half])
-            if half == 1:
-                store(n)
-
         h_at = T * 4
-        first_at = h_at + 2 * HALF * PACK * 2
-        turn_weight()
-        last_terms_at = first_at + 2 * HALF * 4
         load_res(3, "wu_raw1")
-        gate_stage(0)
-        pick(0)
+        weight = tile("weight", [P, J], F32, reuse="wu_bf1")
+        nc.sync.dma_start(out=weight[:], in_=wgo)
         h_bf[0] = tile("h_bf0", [P, HALF * PACK], BF16, reuse=h_at)
-        for c in range(PER_HALF):
-            gate_stage(c + 1)
-            up_stage(c)
-            if c == 1:
-                pick(1)
+        multiply("ga", 0, GATE_BANKS[0])
+        squash(0)
+        pick(0)
+        multiply("ub", 0, UP_BANKS[0])
+        hidden(0)
+        multiply("ub", 1, UP_BANKS[1])
+        multiply("ga", 1, GATE_BANKS[1])
+        squash(1)
+        hidden(1)
+        pick(1)
+        multiply("ub", 2, UP_BANKS[2])
+        multiply("ga", 2, GATE_BANKS[2])
+        squash(2)
+        hidden(2)
+        multiply("ga", 3, GATE_BANKS[3])
+        squash(3)
+        multiply("ub", 3, UP_BANKS[3])
+        hidden(3)
         pick(2)
         h_w[0] = tile("h_w0", [P, HALF], U32, reuse=0)
         quantise_h(0)
-        pick(3, reuse=h_at + 64 - J * 4)
-        h_bf[1] = tile("h_bf1", [P, HALF * PACK], BF16, reuse=h_at + HALF * PACK * 2 - 64)
-        gate_stage(5)
-        up_stage(4)
-        weigh_first(0, turn_residual, 6)
-        gate_stage(6)
-        up_stage(5)
-        up_stage(6)
-        gate_stage(7)
-        up_stage(7)
-        weigh_first(1, second_product, 7)
-        combine(0, 0, 4, reuse=first_at)
-        place(0, 0)
-        hidden(6, reuse="terms0_0")
-        squash(7, reuse=last_terms_at + 64 - CHUNK * PACK * 4)
-        hidden(7, reuse=last_terms_at + 2 * P * 4 - 64)
-        h_w[1] = tile("h_w1", [P, HALF], U32, reuse=first_at)
+        h_bf[1] = tile("h_bf1", [P, HALF * PACK], BF16, reuse=h_at)
+        for c in range(PER_HALF, CHUNKS):
+            multiply("ga", c, GATE_BANKS[c])
+            squash(c)
+            multiply("ub", c, UP_BANKS[c])
+            hidden(c)
+        second_product(0, 0, 6)
+        h_w[1] = tile("h_w1", [P, HALF], U32)
         quantise_h(1)
-        unit(1, 0, (2, 3, 5))
-        place(1, 0)
-        unit(2, 0, (3, 5, 6))
-        place(2, 0)
-        for n in range(3):
-            unit(n, 1, (0, 1, 2) if n % 2 == 0 else (3, 4, 5))
-            place(n, 1)
-        last = tile("total_last", [P, J], F32)
-        for half in range(2):
-            total[3, half] = last[:, half * HALF : (half + 1) * HALF]
-            unit(3, half, (0, 1, 2) if half else (6, 7, 3))
-        nc.vector.tensor_copy(pages[0][:].indirect(offsets[:]), last[:])
-        store(3)
+        pick(3, reuse=h_at + 64 - J * 4)
+        total_at = h_at + HALF * PACK * 2 - 64
+        add_residual(0, 0, reuse=total_at)
+        weigh_and_place(0, 0)
+        for n, half in ((0, 1), (1, 0), (1, 1)):
+            second_product(n, half, 6 + (n + half) % 2)
+            add_residual(n, half, reuse=total_at)
+            weigh_and_place(n, half)
+        for n in (2, 3):
+            for half in range(2):
+                second_product(n, half, half)
+            total[n] = tile("total%d" % n, [P, J], F32, reuse=h_at + 64 if n == 2 else total_at + HALF * 4 - 64)
+            nc.gpsimd.tensor_tensor(total[n][:], picked[n][:], y_whole[n][:], ADD)
+            nc.vector.tensor_tensor(pages[n % 2][:].indirect(offsets[:]), total[n][:], weight[:], MULT)
+            store(n)

@@ -67,7 +67,7 @@ def tile_list_modp_gsigm_res_kernel(
         nc.gpsimd.memset(tab_sc[P // 2 :, :].bitcast(I32), 0)
 
         x_sc = tile("x_sc", [P, PASSES * J], U8)
-        pages = [tile("page%d" % i, [P, T], F32) for i in range(2)]
+        pages = [tile("page%d" % i, [P, T], F32) for i in range(3)]
         nc.vector.memset(pages[0][:], 0.0)
         for page in pages[1:]:
             nc.gpsimd.memset(page[:], 0.0)
@@ -209,8 +209,8 @@ def tile_list_modp_gsigm_res_kernel(
                 nc.scalar.copy(up[:], ub)
                 nc.gpsimd.tensor_tensor(h, up[:], gate[c][:], MULT)
 
-        GATE_BANKS = (0, 1, 2, 1, 0, 1, 0, 2)
-        UP_BANKS = (1, 2, 0, 3, 2, 3, 4, 5)
+        GATE_BANKS = (0, 1, 2, 1, 0, 1, 0, 7)
+        UP_BANKS = (1, 2, 0, 3, 2, 3, 6, 4)
 
         def quantise_h(half):
             nc.vector.quantize_mx(
@@ -223,7 +223,7 @@ def tile_list_modp_gsigm_res_kernel(
             picked[n] = tile("picked%d" % n, [P, J], F32, reuse=reuse)
             nc.vector.tensor_copy(picked[n][:], res[n][:].indirect(offsets[:]))
 
-        y, total = {}, {}
+        y, total, scaled = {}, {}, {}
         y_whole = [tile("y%d" % n, [P, J], F32) for n in range(ROW_BLOCKS)]
 
         def second_product(n, half, number):
@@ -242,19 +242,15 @@ def tile_list_modp_gsigm_res_kernel(
 
         def add_residual(n, half, reuse=None):
             cols = slice(half * HALF, (half + 1) * HALF)
-            if n < 2:
-                total[n, half] = tile("total%d_%d" % (n, half), [P, HALF], F32, reuse=reuse)[:]
-            else:
-                if half == 0:
-                    total[n] = tile("total%d" % n, [P, J], F32, reuse=reuse)
-                total[n, half] = total[n][:, cols]
+            total[n, half] = tile("total%d_%d" % (n, half), [P, HALF], F32, reuse=reuse)[:]
             nc.gpsimd.tensor_tensor(total[n, half], picked[n][:, cols], y[n, half], ADD)
 
-        def weigh_and_place(n, half, reuse=None):
-            cols = slice(half * HALF, (half + 1) * HALF)
-            scaled = tile("scaled%d_%d" % (n, half), [P, HALF], F32, reuse=reuse)
-            nc.gpsimd.tensor_tensor(scaled[:], total[n, half], weight[:, cols], MULT)
-            nc.vector.tensor_copy(pages[n][:].indirect(entries(half * HALF, (half + 1) * HALF)), scaled[:])
+        def weigh(n, half):
+            scaled[n, half] = tile("scaled%d_%d" % (n, half), [P, HALF], F32)
+            nc.gpsimd.tensor_tensor(scaled[n, half][:], total[n, half], weight[:, half * HALF : (half + 1) * HALF], MULT)
+
+        def place(n, half):
+            nc.vector.tensor_copy(pages[n][:].indirect(entries(half * HALF, (half + 1) * HALF)), scaled[n, half][:])
             if half == 1:
                 store(n)
 
@@ -287,27 +283,46 @@ def tile_list_modp_gsigm_res_kernel(
         pick(2)
         h_w[0] = tile("h_w0", [P, HALF], U32, reuse=0)
         quantise_h(0)
-        h_bf[1] = tile("h_bf1", [P, HALF * PACK], BF16, reuse=h_at)
-        for c in range(PER_HALF, CHUNKS):
+        pick(3, reuse=h_at + 64 - J * 4)
+        h1_at = h_at + HALF * PACK * 2 - 64
+        h_bf[1] = tile("h_bf1", [P, HALF * PACK], BF16, reuse=h1_at)
+        for c in (4, 5):
             multiply("ga", c, GATE_BANKS[c])
             squash(c)
             multiply("ub", c, UP_BANKS[c])
             hidden(c)
-        second_product(0, 0, 6)
+        multiply("ga", 6, GATE_BANKS[6])
+        squash(6)
+        for n, number in ((0, UP_BANKS[6]), (1, GATE_BANKS[7]), (2, UP_BANKS[7])):
+            second_product(n, 0, number)
+        multiply("ub", 6, UP_BANKS[6])
+        hidden(6)
+        multiply("ga", 7, GATE_BANKS[7])
+        squash(7)
+        multiply("ub", 7, UP_BANKS[7])
+        hidden(7)
+        add_residual(0, 0)
         h_w[1] = tile("h_w1", [P, HALF], U32)
+        weigh(0, 0)
         quantise_h(1)
-        pick(3, reuse=h_at + 64 - J * 4)
-        total_at = h_at + HALF * PACK * 2 - 64
-        add_residual(0, 0, reuse=total_at)
-        weigh_and_place(0, 0)
-        for n, half in ((0, 1), (1, 0), (1, 1)):
-            second_product(n, half, 6 + (n + half) % 2)
+        place(0, 0)
+        total_at = h1_at + HALF * PACK * 2 - 64
+        add_residual(1, 0, reuse="total0_0")
+        weigh(1, 0)
+        place(1, 0)
+        for n, half in ((2, 0), (0, 1), (1, 1)):
+            if half == 1:
+                second_product(n, half, n)
             add_residual(n, half, reuse=total_at)
-            weigh_and_place(n, half)
-        for n in (2, 3):
-            for half in range(2):
-                second_product(n, half, half)
-            total[n] = tile("total%d" % n, [P, J], F32, reuse=h_at + 64 if n == 2 else total_at + HALF * 4 - 64)
-            nc.gpsimd.tensor_tensor(total[n][:], picked[n][:], y_whole[n][:], ADD)
-            nc.vector.tensor_tensor(pages[n % 2][:].indirect(offsets[:]), total[n][:], weight[:], MULT)
-            store(n)
+            weigh(n, half)
+            place(n, half)
+        second_product(3, 0, 2)
+        second_product(3, 1, 3)
+        last = tile("total3", [P, J], F32, reuse=total_at + HALF * 4 - 64)
+        nc.gpsimd.tensor_tensor(last[:], picked[3][:], y_whole[3][:], ADD)
+        second_product(2, 1, 5)
+        add_residual(2, 1, reuse="y3")
+        nc.vector.tensor_tensor(pages[2][:].indirect(entries(HALF, J)), total[2, 1], weight[:, HALF:], MULT)
+        store(2)
+        nc.vector.tensor_tensor(pages[0][:].indirect(offsets[:]), last[:], weight[:], MULT)
+        store(3)

@@ -33,7 +33,7 @@ CHUNKS = J // CHUNK
 VECTOR_CHUNKS = (5, 6, 7)
 BANK_BYTES = 2048
 PER_HALF = HALF // CHUNK
-TAB_SC_FIRST = QUAD // 2
+TAB_SC_FIRST = QUAD
 
 
 def tile_list_modp_gsigm_res_kernel(
@@ -60,13 +60,15 @@ def tile_list_modp_gsigm_res_kernel(
         wg_sc_raw = tile("wg_sc_raw", [P, PASSES * R], U8, reuse=0)
         nc.gpsimd.memset(wg_sc_raw[:].bitcast(I32), 0)
         tab_sc = tile("tab_sc", [P, T], U8)
-        rows = tab_scales.rearrange("a (h o r) t -> o (a h) r t", h=2, o=2).bitcast(I32)
-        for odd in range(2):
-            nc.gpsimd.memset(tab_sc[QUAD * odd : QUAD * odd + TAB_SC_FIRST, :].bitcast(I32), 0)
-            nc.sync.dma_start(out=tab_sc[QUAD * odd + TAB_SC_FIRST : QUAD * (odd + 1), :].bitcast(I32), in_=rows[odd])
+        nc.gpsimd.memset(tab_sc[:TAB_SC_FIRST, :].bitcast(I32), 0)
+        nc.sync.dma_start(
+            out=tab_sc[TAB_SC_FIRST : 2 * TAB_SC_FIRST, :].bitcast(I32),
+            in_=tab_scales.rearrange("a q t -> q a t").bitcast(I32),
+        )
         nc.gpsimd.memset(tab_sc[P // 2 :, :].bitcast(I32), 0)
 
         x_sc = tile("x_sc", [P, PASSES * J], U8)
+        nc.gpsimd.memset(x_sc[:].bitcast(I32), 0)
         pages = [tile("page%d" % i, [P, T], F32) for i in range(3)]
         nc.vector.memset(pages[0][:], 0.0)
         for page in pages[1:]:
@@ -94,13 +96,12 @@ def tile_list_modp_gsigm_res_kernel(
 
         picked_sc = tile("picked_sc", [P, J], U8)
         nc.vector.tensor_copy(picked_sc[:], tab_sc[:].indirect(offsets[:]))
-        for a in range(PASSES):
-            for upper in range(2):
-                first = TAB_SC_FIRST + SC_ROWS * (2 * a + upper)
-                nc.sync.dma_start(
-                    out=x_sc[P // 2 * upper : P // 2 * (upper + 1), a * J : (a + 1) * J].bitcast(I32),
-                    in_=picked_sc[first : first + P // 2, :].bitcast(I32),
-                )
+        for q in range(QUADS):
+            first = TAB_SC_FIRST + PASSES * SC_ROWS * q
+            nc.sync.dma_start(
+                out=x_sc[QUAD * q : QUAD * q + SC_ROWS, :].rearrange("p (a j) -> p a j", a=PASSES).bitcast(I32),
+                in_=picked_sc[first : first + PASSES * SC_ROWS, :].bitcast(I32),
+            )
 
         both = tile("both", [P, J], U32)
         nc.vector.tensor_copy(both[:], tab_w[:].bitcast(U32).indirect(offsets[:]))

@@ -32,6 +32,7 @@ CHUNK = 128
 CHUNKS = J // CHUNK
 VECTOR_CHUNKS = (5, 6, 7)
 BANK_BYTES = 2048
+QUAD_ORDER = (0, 2, 1, 3)
 PER_HALF = HALF // CHUNK
 TAB_SC_FIRST = QUAD
 
@@ -85,7 +86,7 @@ def tile_list_modp_gsigm_res_kernel(
         nc.sync.dma_start(out=tab_w[:], in_=tab_words[0].rearrange("p t b -> p (t b)").bitcast(I32))
         wg_w_raw = tile("wg_w_raw", [P, PASSES, FP4_BYTES * R], U8)
         nc.sync.dma_start(out=wg_w_raw[:].bitcast(I32), in_=wg_words.rearrange("a p b -> p a b").bitcast(I32))
-        for q in range(QUADS):
+        for q in QUAD_ORDER:
             rows = wg_sc_raw[QUAD * q : QUAD * q + SC_ROWS, :]
             nc.sync.dma_start(
                 out=rows.rearrange("p (a r) -> p a r", a=PASSES).bitcast(I32),
@@ -96,7 +97,7 @@ def tile_list_modp_gsigm_res_kernel(
 
         picked_sc = tile("picked_sc", [P, J], U8)
         nc.vector.tensor_copy(picked_sc[:], tab_sc[:].indirect(offsets[:]))
-        for q in range(QUADS):
+        for q in QUAD_ORDER:
             first = TAB_SC_FIRST + PASSES * SC_ROWS * q
             nc.sync.dma_start(
                 out=x_sc[QUAD * q : QUAD * q + SC_ROWS, :].rearrange("p (a j) -> p a j", a=PASSES).bitcast(I32),
@@ -150,7 +151,7 @@ def tile_list_modp_gsigm_res_kernel(
         nc.sync.dma_start(out=wd_w[:].bitcast(I32), in_=wd_words[0].bitcast(I32))
         wd_sc = tile("wd_sc", [P, N], U8, reuse="wu_bf0")
         nc.gpsimd.memset(wd_sc[:].bitcast(I32), 0)
-        for q in range(QUADS):
+        for q in QUAD_ORDER:
             nc.sync.dma_start(
                 out=wd_sc[QUAD * q : QUAD * q + SC_ROWS, :].bitcast(I32),
                 in_=wd_scales[0, SC_ROWS * q : SC_ROWS * (q + 1), :].bitcast(I32),

from contextlib import ExitStack

import concourse.mybir as mybir

K, R, N, T, J = 1024, 512, 512, 2048, 1024
FLOPS = 2 * (2 * K * R * J + R * N * J)

F32 = mybir.dt.float32
BF16 = mybir.dt.bfloat16
I32 = mybir.dt.int32
U32 = mybir.dt.uint32
U16 = mybir.dt.uint16
U8 = mybir.dt.uint8
FP8X4 = mybir.dt.float8_e4m3fn_x4
FP4X4 = mybir.dt.float4_e2m1fn_x4
MULT = mybir.AluOpType.mult
ADD = mybir.AluOpType.add
SIGMOID = mybir.ActivationFunctionType.Sigmoid

P = 128
PACK = 4
K_PASS = P * PACK
PASSES = K // K_PASS
QUAD = 32
QUADS = P // QUAD
SC_ROWS = 4
FP4_BYTES = 2
LIST_ROWS = 16
ROW_BLOCKS = N // P
HALF = J // 2
CHUNK = 128
CHUNKS = J // CHUNK
VECTOR_CHUNKS = (5, 6, 7)
BANK_BYTES = 2048
QUAD_ORDER = (0, 2, 1, 3)
PER_HALF = HALF // CHUNK
TAB_SC_FIRST = QUAD


def tile_list_modp_gsigm_res_kernel(
    tc, tab_words, tab_scales, wg_words, wg_scales, wu, wd_words, wd_scales, rT, wgo, offs, out
):
    nc = tc.nc
    with ExitStack() as ctx:
        keep = ctx.enter_context(tc.tile_pool(name="keep", bufs=1))
        psum = ctx.enter_context(tc.psum_pool(name="psum", bufs=1))

        shared = ctx.enter_context(tc.tile_pool(name="shared", bufs=1))

        def tile(name, shape, dtype, reuse=None):
            if isinstance(reuse, int):
                return shared.tile(shape, dtype, name=name, offset=reuse, align_bytes=64)
            return keep.tile(shape, dtype, name=name, tag=reuse or name, align_bytes=64)

        offsets = keep.tile([P, J // LIST_ROWS], U16, name="offsets")
        nc.sync.dma_start(offsets[:], offs)

        def entries(j0, j1):
            return offsets[:, j0 // LIST_ROWS : j1 // LIST_ROWS]

        wg_sc_raw = tile("wg_sc_raw", [P, PASSES * R], U8, reuse=0)
        nc.gpsimd.memset(wg_sc_raw[:].bitcast(I32), 0)
        tab_sc = tile("tab_sc", [P, T], U8)
        nc.gpsimd.memset(tab_sc[:TAB_SC_FIRST, :].bitcast(I32), 0)
        nc.sync.dma_start(
            out=tab_sc[TAB_SC_FIRST : 2 * TAB_SC_FIRST, :].bitcast(I32),
            in_=tab_scales.rearrange("a q t -> q a t").bitcast(I32),
        )
        nc.gpsimd.memset(tab_sc[P // 2 :, :].bitcast(I32), 0)

        x_sc = tile("x_sc", [P, PASSES * J], U8)
        nc.gpsimd.memset(x_sc[:].bitcast(I32), 0)
        pages = [tile("page%d" % i, [P, T], F32) for i in range(3)]
        nc.vector.memset(pages[0][:], 0.0)
        for page in pages[1:]:
            nc.gpsimd.memset(page[:], 0.0)

        wu_raw = []

        def load_wu(a):
            wu_raw.append(tile("wu_raw%d" % a, [P, PACK, R], F32))
            rows = wu[K_PASS * a : K_PASS * (a + 1), :]
            nc.sync.dma_start(out=wu_raw[a][:], in_=rows.rearrange("(p i) r -> p i r", i=PACK))

        tab_w = tile("tab_w", [P, T], I32)
        nc.sync.dma_start(out=tab_w[:], in_=tab_words[0].rearrange("p t b -> p (t b)").bitcast(I32))
        wg_w_raw = tile("wg_w_raw", [P, PASSES, FP4_BYTES * R], U8)
        nc.sync.dma_start(out=wg_w_raw[:].bitcast(I32), in_=wg_words.rearrange("a p b -> p a b").bitcast(I32))
        for q in QUAD_ORDER:
            rows = wg_sc_raw[QUAD * q : QUAD * q + SC_ROWS, :]
            nc.sync.dma_start(
                out=rows.rearrange("p (a r) -> p a r", a=PASSES).bitcast(I32),
                in_=wg_scales[:, SC_ROWS * q : SC_ROWS * (q + 1), :].rearrange("a q r -> q a r").bitcast(I32),
            )
        for a in range(PASSES):
            load_wu(a)

        picked_sc = tile("picked_sc", [P, J], U8)
        nc.vector.tensor_copy(picked_sc[:], tab_sc[:].indirect(offsets[:]))
        for q in QUAD_ORDER:
            first = TAB_SC_FIRST + PASSES * SC_ROWS * q
            nc.sync.dma_start(
                out=x_sc[QUAD * q : QUAD * q + SC_ROWS, :].rearrange("p (a j) -> p a j", a=PASSES).bitcast(I32),
                in_=picked_sc[first : first + PASSES * SC_ROWS, :].bitcast(I32),
            )

        both = tile("both", [P, J], U32)
        nc.vector.tensor_copy(both[:], tab_w[:].bitcast(U32).indirect(offsets[:]))
        x_w = tile("x_w", [P, PASSES * FP4_BYTES * J], U8)
        nc.vector.tensor_copy(
            x_w[:].bitcast(U16).rearrange("p (a j) -> p a j", a=PASSES),
            both[:].bitcast(U16).rearrange("p (j a) -> p a j", a=PASSES),
        )

        wg_w = tile("wg_w", [P, PASSES * FP4_BYTES * R], U8)
        nc.vector.tensor_copy(
            wg_w[:].bitcast(U16).rearrange("p (a t m) -> p a t m", a=PASSES, t=PACK),
            wg_w_raw[:].bitcast(U16).rearrange("p a (m t) -> p a t m", t=PACK),
        )
        wg_sc = tile("wg_sc", [P, PASSES * R], U8)
        nc.vector.tensor_copy(
            wg_sc[:].rearrange("p (a t m) -> p a t m", a=PASSES, t=PACK),
            wg_sc_raw[:].rearrange("p (a m t) -> p a t m", a=PASSES, t=PACK),
        )

        wu_w, wu_sc = [], []
        for a in range(PASSES):
            wu_bf = tile("wu_bf%d" % a, [P, PACK * R], BF16)
            by_slot = wu_bf[:].rearrange("p (t m i) -> p m t i", t=PACK, i=PACK)
            source = wu_raw[a][:].rearrange("p i (m t) -> p m t i", t=PACK)
            if a < PASSES - 1:
                nc.scalar.copy(by_slot, source)
            else:
                nc.scalar.copy(by_slot[:, : P // 2], source[:, : P // 2])
                nc.vector.tensor_copy(by_slot[:, P // 2 :], source[:, P // 2 :])
            wu_w.append(tile("wu_w%d" % a, [P, R], U32))
            wu_sc.append(tile("wu_sc%d" % a, [P, R], U8))
            nc.vector.quantize_mx(out=wu_w[a][:].bitcast(FP8X4), scales=wu_sc[a][:], in_=wu_bf[:])


        res = []

        def load_res(n, reuse):
            res.append(tile("res%d" % n, [P, T], F32, reuse=reuse))
            nc.sync.dma_start(out=res[n][:], in_=rT[n * P : (n + 1) * P, :])

        load_res(0, "tab_sc")
        load_res(1, "both")
        load_res(2, 0)
        wd_w = tile("wd_w", [P, FP4_BYTES * N], U8, reuse="wu_raw0")
        nc.sync.dma_start(out=wd_w[:].bitcast(I32), in_=wd_words[0].bitcast(I32))
        wd_sc = tile("wd_sc", [P, N], U8, reuse="wu_bf0")
        nc.gpsimd.memset(wd_sc[:].bitcast(I32), 0)
        for q in QUAD_ORDER:
            nc.sync.dma_start(
                out=wd_sc[QUAD * q : QUAD * q + SC_ROWS, :].bitcast(I32),
                in_=wd_scales[0, SC_ROWS * q : SC_ROWS * (q + 1), :].bitcast(I32),
            )

        def first_product(bank, c, words, scales):
            for a in range(PASSES):
                b0 = FP4_BYTES * (a * J + c * CHUNK)
                for t in range(PACK):
                    nc.tensor.matmul_mx(
                        out=bank[:, t, :],
                        lhsT=words(a, t),
                        lhsT_scale=scales(a, t),
                        rhs=x_w[:, b0 : b0 + FP4_BYTES * CHUNK].bitcast(FP4X4),
                        rhs_scale=x_sc[:, a * J + c * CHUNK : a * J + (c + 1) * CHUNK],
                        start=(a == 0 and t == 0),
                        stop=(a == PASSES - 1 and t == PACK - 1),
                    )

        h_w, h_bf = {}, {}
        h_sc = tile("h_sc", [P, J], U8)

        def bank(name, shape, number):
            return psum.tile(shape, F32, name=name, offset=number * BANK_BYTES)

        gate, sums = {}, {}

        def multiply(kind, c, number):
            sums[kind, c] = bank("%s%d" % (kind, c), [P, PACK, CHUNK], number)
            if kind == "ga":
                first_product(
                    sums[kind, c],
                    c,
                    lambda a, t: wg_w[:, FP4_BYTES * (a * R + t * P) : FP4_BYTES * (a * R + (t + 1) * P)].bitcast(FP4X4),
                    lambda a, t: wg_sc[:, a * R + t * P : a * R + (t + 1) * P],
                )
            else:
                first_product(
                    sums[kind, c],
                    c,
                    lambda a, t: wu_w[a][:, t * P : (t + 1) * P].bitcast(FP8X4),
                    lambda a, t: wu_sc[a][:, t * P : (t + 1) * P],
                )

        def squash(c, reuse=None):
            gate[c] = tile("gate%d" % c, [P, CHUNK, PACK], F32, reuse=reuse)
            nc.scalar.activation(gate[c][:], sums["ga", c][:].rearrange("p t j -> p j t"), SIGMOID)

        def hidden(c, reuse=None):
            half, j0 = divmod(c * CHUNK, HALF)
            h = h_bf[half][:, j0 * PACK : (j0 + CHUNK) * PACK].rearrange("p (j t) -> p j t", t=PACK)
            ub = sums["ub", c][:].rearrange("p t j -> p j t")
            if c in VECTOR_CHUNKS:
                nc.vector.tensor_tensor(h, ub, gate[c][:], MULT)
            else:
                up = tile("up%d" % c, [P, CHUNK, PACK], F32, reuse=reuse)
                nc.scalar.copy(up[:], ub)
                nc.gpsimd.tensor_tensor(h, up[:], gate[c][:], MULT)

        GATE_BANKS = (0, 1, 2, 1, 0, 1, 0, 7)
        UP_BANKS = (1, 2, 0, 3, 2, 3, 6, 4)

        def quantise_h(half):
            nc.vector.quantize_mx(
                out=h_w[half][:].bitcast(FP8X4), scales=h_sc[:, half * HALF : (half + 1) * HALF], in_=h_bf[half][:]
            )

        picked = {}

        def pick(n, reuse=None):
            picked[n] = tile("picked%d" % n, [P, J], F32, reuse=reuse)
            nc.vector.tensor_copy(picked[n][:], res[n][:].indirect(offsets[:]))

        y, total, scaled = {}, {}, {}
        y_whole = [tile("y%d" % n, [P, J], F32) for n in range(ROW_BLOCKS)]

        def second_product(n, half, number):
            acc = bank("y%d_%d" % (n, half), [P, HALF], number)
            nc.tensor.matmul_mx(
                out=acc[:],
                lhsT=wd_w[:, FP4_BYTES * n * P : FP4_BYTES * (n + 1) * P].bitcast(FP4X4),
                lhsT_scale=wd_sc[:, n * P : (n + 1) * P],
                rhs=h_w[half][:].bitcast(FP8X4),
                rhs_scale=h_sc[:, half * HALF : (half + 1) * HALF],
                start=True,
                stop=True,
            )
            y[n, half] = y_whole[n][:, half * HALF : (half + 1) * HALF]
            nc.scalar.copy(y[n, half], acc[:])

        def add_residual(n, half, reuse=None):
            cols = slice(half * HALF, (half + 1) * HALF)
            total[n, half] = tile("total%d_%d" % (n, half), [P, HALF], F32, reuse=reuse)[:]
            nc.gpsimd.tensor_tensor(total[n, half], picked[n][:, cols], y[n, half], ADD)

        def weigh(n, half):
            scaled[n, half] = tile("scaled%d_%d" % (n, half), [P, HALF], F32)
            nc.gpsimd.tensor_tensor(scaled[n, half][:], total[n, half], weight[:, half * HALF : (half + 1) * HALF], MULT)

        def place(n, half):
            nc.vector.tensor_copy(pages[n][:].indirect(entries(half * HALF, (half + 1) * HALF)), scaled[n, half][:])
            if half == 1:
                store(n)

        def store(n):
            nc.sync.dma_start(out=out[n * P : (n + 1) * P, :], in_=pages[n % len(pages)][:])

        h_at = T * 4
        load_res(3, "wu_raw1")
        weight = tile("weight", [P, J], F32, reuse="wu_bf1")
        nc.sync.dma_start(out=weight[:], in_=wgo)
        h_bf[0] = tile("h_bf0", [P, HALF * PACK], BF16, reuse=h_at)
        multiply("ga", 0, GATE_BANKS[0])
        squash(0)
        pick(0)
        multiply("ub", 0, UP_BANKS[0])
        hidden(0)
        multiply("ub", 1, UP_BANKS[1])
        multiply("ga", 1, GATE_BANKS[1])
        squash(1)
        hidden(1)
        pick(1)
        multiply("ub", 2, UP_BANKS[2])
        multiply("ga", 2, GATE_BANKS[2])
        squash(2)
        hidden(2)
        multiply("ga", 3, GATE_BANKS[3])
        squash(3)
        multiply("ub", 3, UP_BANKS[3])
        hidden(3)
        pick(2)
        h_w[0] = tile("h_w0", [P, HALF], U32, reuse=0)
        quantise_h(0)
        pick(3, reuse=h_at + 64 - J * 4)
        h1_at = h_at + HALF * PACK * 2 - 64
        h_bf[1] = tile("h_bf1", [P, HALF * PACK], BF16, reuse=h1_at)
        for c in (4, 5):
            multiply("ga", c, GATE_BANKS[c])
            squash(c)
            multiply("ub", c, UP_BANKS[c])
            hidden(c)
        multiply("ga", 6, GATE_BANKS[6])
        squash(6)
        for n, number in ((0, UP_BANKS[6]), (1, GATE_BANKS[7]), (2, UP_BANKS[7])):
            second_product(n, 0, number)
        multiply("ub", 6, UP_BANKS[6])
        hidden(6)
        multiply("ga", 7, GATE_BANKS[7])
        squash(7)
        multiply("ub", 7, UP_BANKS[7])
        hidden(7)
        add_residual(0, 0)
        h_w[1] = tile("h_w1", [P, HALF], U32)
        weigh(0, 0)
        quantise_h(1)
        place(0, 0)
        total_at = h1_at + HALF * PACK * 2 - 64
        add_residual(1, 0, reuse="total0_0")
        weigh(1, 0)
        place(1, 0)
        for n, half in ((2, 0), (0, 1), (1, 1)):
            if half == 1:
                second_product(n, half, n)
            add_residual(n, half, reuse=total_at)
            weigh(n, half)
            place(n, half)
        second_product(3, 0, 2)
        second_product(3, 1, 3)
        last = tile("total3", [P, J], F32, reuse=total_at + HALF * 4 - 64)
        nc.gpsimd.tensor_tensor(last[:], picked[3][:], y_whole[3][:], ADD)
        second_product(2, 1, 5)
        add_residual(2, 1, reuse="y3")
        nc.vector.tensor_tensor(pages[2][:].indirect(entries(HALF, J)), total[2, 1], weight[:, HALF:], MULT)
        store(2)
        nc.vector.tensor_tensor(pages[0][:].indirect(offsets[:]), last[:], weight[:], MULT)
        store(3)
